import numpy as np
import ml_dtypes


def mxq(x, axis, fmt="e4m3"):
    dtype, down = {"e4m3": (ml_dtypes.float8_e4m3fn, 7), "e5m2": (ml_dtypes.float8_e5m2, 14)}[fmt]
    v = np.moveaxis(np.asarray(x, np.float32).astype(ml_dtypes.bfloat16).astype(np.float64), axis, -1)
    blocks = v.reshape(v.shape[:-1] + (-1, 32))
    amax = np.abs(blocks).max(-1, keepdims=True)
    byte = np.maximum(np.where(amax > 0, np.frexp(amax)[1] - 1 + 127, 0) - down, 1)
    scale = np.exp2(byte - 127.0)
    codes = (blocks / scale).astype(np.float32).astype(dtype).astype(np.float64)
    return np.moveaxis((codes * scale).reshape(v.shape), -1, axis)


WIDE = False


def mx_kscale(k):
    if not WIDE:
        return np.ones(k)
    levels = np.array([10, -10, 5, -5, 0])
    if k % 512:
        return np.exp2(np.random.permutation(np.resize(levels, k // 32))).repeat(32)
    a = np.empty((k // 512, 16))
    for p in range(k // 512):
        a[p, :8] = np.random.permutation(np.resize(levels, 8))
        for g in range(8):
            far = levels[np.abs(levels - a[p, g]) >= 10]
            a[p, g + 8] = far[np.random.randint(len(far))]
    return np.exp2(a.ravel()).repeat(32)


def f64(x):
    return np.asarray(x).astype(np.float64)


def striped(idx):
    return np.tile(idx.reshape(-1, 16).T, (8, 1)).astype(np.uint16)


def unstriped(offs):
    return offs[:16].T.reshape(-1).astype(np.int64)


def pack_weight(w):
    k, n = w.shape
    w = f64(np.asarray(w, np.float32).astype(ml_dtypes.bfloat16)).reshape(k // 32, 32, n)
    amax = np.abs(w).max(1)
    byte = np.clip(np.where(amax > 0, np.frexp(amax)[1] - 1 + 127 - 7, 1), 1, 254)
    scaled = (w * np.exp2(127.0 - byte)[:, None, :]).reshape(k, n).astype(np.float32)
    words = np.ascontiguousarray(scaled.reshape(k // 512, 128, 4, n).transpose(0, 1, 3, 2)).astype(ml_dtypes.float8_e4m3fn).view(np.uint8)
    return words, np.ascontiguousarray(byte.astype(np.uint8).reshape(k // 512, 16, n))


def unpack_weight(words, scales):
    g, p, n, _ = words.shape
    vals = np.ascontiguousarray(words).view(ml_dtypes.float8_e4m3fn).astype(np.float64) * np.repeat(np.exp2(scales.astype(np.float64) - 127.0), 8, axis=1)[..., None]
    return vals.transpose(0, 1, 3, 2).reshape(g * 512, n)


def relu(v):
    return np.maximum(v, 0.0)


K, T, S, V, H, N = 512, 4096, 1024, 512, 512, 128


def setup_inputs():
    n = np.random.standard_normal
    s = mx_kscale(K)[:, None]
    u = mx_kscale(H)
    packed_xT = pack_weight(n((K, T)) * s)
    packed_w2 = pack_weight(n((H, N)) / np.sqrt(2 * H) / u[:, None])
    packed_w3 = pack_weight(n((H, N)) / np.sqrt(2 * H) / u[:, None])
    return {
        "x_words": packed_xT[0],
        "x_scales": packed_xT[1],
        "w1": (n((K, H)) / np.sqrt(K) / s * u).astype(np.float32),
        "w2_words": packed_w2[0],
        "w2_scales": packed_w2[1],
        "w3_words": packed_w3[0],
        "w3_scales": packed_w3[1],
        "offs": striped(np.random.permutation(T)[:S]),
        "cen": striped(np.random.permutation(S)[:V]),
        "pos1": striped(np.random.permutation(S)[:V]),
        "pos2": striped(np.random.permutation(S)[:V]),
        "pos3": striped(np.random.permutation(S)[:V]),
    }


def reference(x_words, x_scales, w1, w2_words, w2_scales, w3_words, w3_scales, offs, cen, pos1, pos2, pos3):
    xq = unpack_weight(x_words, x_scales)[:, unstriped(offs)]
    h = relu(mxq(f64(w1), 0, "e4m3").T @ xq)
    hc = h[:, unstriped(cen)]
    z = np.maximum(np.maximum(h[:, unstriped(pos1)], h[:, unstriped(pos2)]), h[:, unstriped(pos3)])
    return unpack_weight(w2_words, w2_scales).T @ mxq(hc, 0, "e4m3") + unpack_weight(w3_words, w3_scales).T @ mxq(z, 0, "e4m3")

@@ -1,0 +1,176 @@
+from contextlib import ExitStack
+
+import concourse.mybir as mybir
+
+K, T, S, V, H, N = 512, 4096, 1024, 512, 512, 128
+FLOPS = 2 * K * H * S + 2 * 2 * H * N * V
+
+F32 = mybir.dt.float32
+BF16 = mybir.dt.bfloat16
+I32 = mybir.dt.int32
+U32 = mybir.dt.uint32
+U16 = mybir.dt.uint16
+U8 = mybir.dt.uint8
+FP8X4 = mybir.dt.float8_e4m3fn_x4
+MAX = mybir.AluOpType.max
+COPY = mybir.ActivationFunctionType.Copy
+RELU = mybir.ActivationFunctionType.Relu
+
+P = 128
+PACK = 4
+QUADS = 4
+LIST_ROWS = 16
+BANK = 512
+CHUNKS = ((0, 256), (256, 384), (384, 512))
+
+
+def tile_picked_sagecat_max_p_kernel(
+    tc, x_words, x_scales, w1, w2_words, w2_scales, w3_words, w3_scales, offs, cen, pos1, pos2, pos3, out
+):
+    nc = tc.nc
+    with ExitStack() as ctx:
+        keep = ctx.enter_context(tc.tile_pool(name="keep", bufs=1))
+        psum_h = ctx.enter_context(tc.psum_pool(name="psum_h", bufs=5))
+        psum_out = ctx.enter_context(tc.psum_pool(name="psum_out", bufs=1))
+
+        def load_list(name, source):
+            tile = keep.tile(list(source.shape), U16, name=name)
+            nc.sync.dma_start(tile[:], source)
+            return tile
+
+        def entries(tile, lo, hi):
+            return tile[:, lo // LIST_ROWS : hi // LIST_ROWS]
+
+        scale_table = keep.tile([P, T], U8, name="scale_table")
+        nc.sync.dma_start(scale_table[P - 16 : P, :].bitcast(I32), x_scales[0].bitcast(I32))
+        nc.vector.memset(scale_table[0 : P - 16, :].bitcast(I32), 0)
+        offs_sb = load_list("offs_sb", offs)
+        x_table = keep.tile([P, T], U32, name="x_table")
+        nc.sync.dma_start(x_table[:].bitcast(I32), x_words[0].rearrange("p n j -> p (n j)").bitcast(I32))
+        pos_sb = [load_list("pos%d_sb" % d, source) for d, source in enumerate((pos1, pos2, pos3))]
+        cen_sb = load_list("cen_sb", cen)
+        w1_raw = keep.tile([P, PACK, H], F32, name="w1_raw")
+        nc.sync.dma_start(w1_raw[:], w1.rearrange("(p j) c -> p j c", j=PACK))
+
+        x_plane = keep.tile([P, S], U8, name="x_plane", align_bytes=64)
+        nc.vector.memset(x_plane[:].bitcast(I32), 0)
+
+        tail_weights = []
+        for name, words, scales in (("w3", w3_words, w3_scales), ("w2", w2_words, w2_scales)):
+            codes = keep.tile([P, N], U32, name=name + "_codes", align_bytes=64)
+            plane = keep.tile([P, N], U8, name=name + "_plane", align_bytes=64)
+            nc.gpsimd.memset(plane[:].bitcast(I32), 0)
+            nc.gpsimd.dma_start(codes[:].bitcast(I32), words[0].rearrange("p n j -> p (n j)").bitcast(I32))
+            for q in range(QUADS):
+                nc.gpsimd.dma_start(plane[32 * q : 32 * q + 4, :].bitcast(I32), scales[0, 4 * q : 4 * q + 4, :].bitcast(I32))
+            tail_weights.append((codes, plane))
+
+        picked_scales = keep.tile([P, S], U8, name="picked_scales")
+        nc.vector.tensor_copy(picked_scales[:], scale_table[:].indirect(offs_sb[:]))
+        for q in range(QUADS):
+            nc.scalar.dma_start(
+                x_plane[32 * q : 32 * q + 4, :].bitcast(I32), picked_scales[P - 16 + 4 * q : P - 12 + 4 * q, :].bitcast(I32)
+            )
+        x_codes = []
+        for half in range(S // BANK):
+            codes = keep.tile([P, BANK], U32, name="x_codes%d" % half, align_bytes=64)
+            nc.vector.tensor_copy(codes[:], x_table[:].indirect(entries(offs_sb, half * BANK, (half + 1) * BANK)))
+            x_codes.append(codes)
+
+        w1_view = w1_raw[:].rearrange("p j (m t) -> p m t j", t=PACK)
+        w1_dealt = [keep.tile([P, 2, P, PACK], BF16, name="w1_dealt%d" % u, align_bytes=64) for u in range(2)]
+        nc.vector.tensor_copy(w1_dealt[0][:].rearrange("p t m j -> p m t j"), w1_view[:, :, 0:2, :])
+        nc.scalar.activation(w1_dealt[1][:].rearrange("p t m j -> p m t j"), w1_view[:, :, 2:4, :], COPY)
+        w1_codes = [keep.tile([P, P], U32, name="w1_codes%d" % t, align_bytes=64) for t in range(PACK)]
+        w1_planes = [keep.tile([P, P], U8, name="w1_plane%d" % t, align_bytes=64) for t in range(PACK)]
+        for t in range(PACK):
+            nc.vector.quantize_mx(
+                w1_codes[t][:].bitcast(FP8X4), w1_planes[t][:], w1_dealt[t // 2][:, t % 2].rearrange("p m j -> p (m j)")
+            )
+
+        h = [keep.tile([P, S], F32, name="h%d" % t) for t in range(PACK)]
+        for t in range(PACK):
+            width = BANK // 2 if t == 0 else BANK
+            for piece, lo in enumerate(range(0, S, width)):
+                acc = psum_h.tile([P, width], F32, name="acc")
+                nc.tensor.matmul_mx(
+                    acc[:],
+                    lhsT=w1_codes[t][:].bitcast(FP8X4),
+                    lhsT_scale=w1_planes[t][:],
+                    rhs=x_codes[lo // BANK][:, lo % BANK : lo % BANK + width].bitcast(FP8X4),
+                    rhs_scale=x_plane[:, lo : lo + width],
+                    start=True,
+                    stop=True,
+                )
+                if t == 0 and piece % 2 == 1:
+                    nc.vector.tensor_scalar_max(h[t][:, lo : lo + width], acc[:], 0.0)
+                else:
+                    nc.scalar.activation(h[t][:, lo : lo + width], acc[:], RELU)
+
+        def interleave(name, planes, width):
+            grouped = keep.tile([P, width, PACK], BF16, name=name + "_grouped", align_bytes=64)
+            nc.scalar.copy(
+                grouped[:].rearrange("p (c i) t -> p c t i", i=4), planes[:].rearrange("p t (c i) -> p c t i", i=4)
+            )
+            return grouped
+
+        def quantize(name, grouped, width):
+            codes = keep.tile([P, width], U32, name=name + "_codes", align_bytes=64)
+            plane = keep.tile([P, width], U8, name=name + "_plane", align_bytes=64)
+            nc.vector.quantize_mx(codes[:].bitcast(FP8X4), plane[:], grouped[:].rearrange("p v t -> p (v t)"))
+            return codes, plane
+
+        nbr = [keep.tile([P, PACK, V], BF16, name="nbr%d" % d) for d in range(3)]
+        z = keep.tile([P, PACK, V], BF16, name="z")
+        own = [keep.tile([P, PACK, hi - lo], BF16, name="own%d" % c) for c, (lo, hi) in enumerate(CHUNKS)]
+
+        def fetch_nbr(d, t):
+            nc.vector.tensor_copy(nbr[d][:, t, :], h[t][:].indirect(pos_sb[d][:]))
+
+        def fetch_own(c, t):
+            nc.vector.tensor_copy(own[c][:, t, :], h[t][:].indirect(entries(cen_sb, *CHUNKS[c])))
+
+        def max_first(u):
+            nc.vector.tensor_tensor(z[:, 2 * u : 2 * u + 2, :], nbr[0][:, 2 * u : 2 * u + 2, :], nbr[1][:, 2 * u : 2 * u + 2, :], MAX)
+
+        def max_last(u):
+            nc.vector.tensor_tensor(z[:, 2 * u : 2 * u + 2, :], z[:, 2 * u : 2 * u + 2, :], nbr[2][:, 2 * u : 2 * u + 2, :], MAX)
+
+        for t in (0, 1):
+            for d in range(3):
+                fetch_nbr(d, t)
+        fetch_nbr(0, 2)
+        max_first(0)
+        fetch_nbr(1, 2)
+        max_last(0)
+        fetch_nbr(2, 2)
+        for d in range(3):
+            fetch_nbr(d, 3)
+        max_first(1)
+        fetch_own(0, 0)
+        max_last(1)
+        z_grouped = interleave("z", z, V)
+        for t in range(1, PACK):
+            fetch_own(0, t)
+        own_grouped = [interleave("own0", own[0], 256)]
+        for c in range(1, len(CHUNKS)):
+            for t in range(PACK):
+                fetch_own(c, t)
+            own_grouped.append(interleave("own%d" % c, own[c], 128))
+        z_codes, z_plane = quantize("z", z_grouped, V)
+
+        (w3_codes, w3_plane), (w2_codes, w2_plane) = tail_weights
+        for c, (lo, hi) in enumerate(CHUNKS):
+            own_codes, own_plane = quantize("own%d" % c, own_grouped[c], hi - lo)
+            acc = psum_out.tile([P, hi - lo], F32, name="out_acc%d" % c)
+            nc.tensor.matmul_mx(
+                acc[:], lhsT=w3_codes[:].bitcast(FP8X4), lhsT_scale=w3_plane[:],
+                rhs=z_codes[:, lo:hi].bitcast(FP8X4), rhs_scale=z_plane[:, lo:hi], start=True, stop=False,
+            )
+            nc.tensor.matmul_mx(
+                acc[:], lhsT=w2_codes[:].bitcast(FP8X4), lhsT_scale=w2_plane[:],
+                rhs=own_codes[:].bitcast(FP8X4), rhs_scale=own_plane[:], start=False, stop=True,
+            )
+            result = keep.tile([P, hi - lo], F32, name="result%d" % c)
+            nc.scalar.copy(result[:], acc[:])
+            nc.sync.dma_start(out[:, lo:hi], result[:])

@@ -45,25 +45,16 @@ def tile_picked_sagecat_max_p_kernel(
         nc.sync.dma_start(scale_table[P - 16 : P, :].bitcast(I32), x_scales[0].bitcast(I32))
         nc.vector.memset(scale_table[0 : P - 16, :].bitcast(I32), 0)
         offs_sb = load_list("offs_sb", offs)
+        pos_sb = [load_list("pos%d_sb" % d, source) for d, source in enumerate((pos1, pos2))]
         x_table = keep.tile([P, T], U32, name="x_table")
         nc.sync.dma_start(x_table[:].bitcast(I32), x_words[0].rearrange("p n j -> p (n j)").bitcast(I32))
-        pos_sb = [load_list("pos%d_sb" % d, source) for d, source in enumerate((pos1, pos2, pos3))]
+        pos_sb.append(load_list("pos2_sb", pos3))
         cen_sb = load_list("cen_sb", cen)
-        w1_raw = keep.tile([P, PACK, H], F32, name="w1_raw")
+        w1_raw = keep.tile([P, PACK, H], F32, name="w1_raw", tag="raw", align_bytes=64)
         nc.sync.dma_start(w1_raw[:], w1.rearrange("(p j) c -> p j c", j=PACK))
 
         x_plane = keep.tile([P, S], U8, name="x_plane", align_bytes=64)
-        nc.vector.memset(x_plane[:].bitcast(I32), 0)
-
-        tail_weights = []
-        for name, words, scales in (("w3", w3_words, w3_scales), ("w2", w2_words, w2_scales)):
-            codes = keep.tile([P, N], U32, name=name + "_codes", align_bytes=64)
-            plane = keep.tile([P, N], U8, name=name + "_plane", align_bytes=64)
-            nc.gpsimd.memset(plane[:].bitcast(I32), 0)
-            nc.gpsimd.dma_start(codes[:].bitcast(I32), words[0].rearrange("p n j -> p (n j)").bitcast(I32))
-            for q in range(QUADS):
-                nc.gpsimd.dma_start(plane[32 * q : 32 * q + 4, :].bitcast(I32), scales[0, 4 * q : 4 * q + 4, :].bitcast(I32))
-            tail_weights.append((codes, plane))
+        nc.gpsimd.memset(x_plane[:].bitcast(I32), 0)
 
         picked_scales = keep.tile([P, S], U8, name="picked_scales")
         nc.vector.tensor_copy(picked_scales[:], scale_table[:].indirect(offs_sb[:]))
@@ -78,7 +69,7 @@ def tile_picked_sagecat_max_p_kernel(
             x_codes.append(codes)
 
         w1_view = w1_raw[:].rearrange("p j (m t) -> p m t j", t=PACK)
-        w1_dealt = [keep.tile([P, 2, P, PACK], BF16, name="w1_dealt%d" % u, align_bytes=64) for u in range(2)]
+        w1_dealt = [keep.tile([P, 2, P, PACK], BF16, name="w1_dealt%d" % u, tag="dealt%d" % u, align_bytes=64) for u in range(2)]
         nc.vector.tensor_copy(w1_dealt[0][:].rearrange("p t m j -> p m t j"), w1_view[:, :, 0:2, :])
         nc.scalar.activation(w1_dealt[1][:].rearrange("p t m j -> p m t j"), w1_view[:, :, 2:4, :], COPY)
         w1_codes = [keep.tile([P, P], U32, name="w1_codes%d" % t, align_bytes=64) for t in range(PACK)]
@@ -88,10 +79,20 @@ def tile_picked_sagecat_max_p_kernel(
                 w1_codes[t][:].bitcast(FP8X4), w1_planes[t][:], w1_dealt[t // 2][:, t % 2].rearrange("p m j -> p (m j)")
             )
 
+        tail_codes = keep.tile([P, 2, N], U32, name="tail_codes", tag="raw", align_bytes=64)
+        tail_planes = keep.tile([P, 2, N], U8, name="tail_planes", tag="dealt0", align_bytes=64)
+        nc.gpsimd.memset(tail_planes[:].rearrange("p w n -> p (w n)").bitcast(I32), 0)
+        for w, (words, scales) in enumerate(((w3_words, w3_scales), (w2_words, w2_scales))):
+            nc.sync.dma_start(tail_codes[:, w, :].bitcast(I32), words[0].rearrange("p n j -> p (n j)").bitcast(I32))
+            for q in range(QUADS):
+                nc.sync.dma_start(
+                    tail_planes[32 * q : 32 * q + 4, w, :].bitcast(I32), scales[0, 4 * q : 4 * q + 4, :].bitcast(I32)
+                )
+
         h = [keep.tile([P, S], F32, name="h%d" % t) for t in range(PACK)]
         for t in range(PACK):
-            width = BANK // 2 if t == 0 else BANK
-            for piece, lo in enumerate(range(0, S, width)):
+            lo = 0
+            for piece, width in enumerate((256, 256, 256, 128, 128) if t == 0 else (BANK, BANK)):
                 acc = psum_h.tile([P, width], F32, name="acc")
                 nc.tensor.matmul_mx(
                     acc[:],
@@ -106,11 +107,12 @@ def tile_picked_sagecat_max_p_kernel(
                     nc.vector.tensor_scalar_max(h[t][:, lo : lo + width], acc[:], 0.0)
                 else:
                     nc.scalar.activation(h[t][:, lo : lo + width], acc[:], RELU)
+                lo = lo + width
 
         def interleave(name, planes, width):
             grouped = keep.tile([P, width, PACK], BF16, name=name + "_grouped", align_bytes=64)
             nc.scalar.copy(
-                grouped[:].rearrange("p (c i) t -> p c t i", i=4), planes[:].rearrange("p t (c i) -> p c t i", i=4)
+                grouped[:].rearrange("p (c i) t -> p c t i", i=4), planes.rearrange("p t (c i) -> p c t i", i=4)
             )
             return grouped
 
@@ -124,51 +126,61 @@ def tile_picked_sagecat_max_p_kernel(
         z = keep.tile([P, PACK, V], BF16, name="z")
         own = [keep.tile([P, PACK, hi - lo], BF16, name="own%d" % c) for c, (lo, hi) in enumerate(CHUNKS)]
 
-        def fetch_nbr(d, t):
-            nc.vector.tensor_copy(nbr[d][:, t, :], h[t][:].indirect(pos_sb[d][:]))
+        def fetch_nbr(d, t, lo, hi):
+            nc.vector.tensor_copy(nbr[d][:, t, lo:hi], h[t][:].indirect(entries(pos_sb[d], lo, hi)))
 
         def fetch_own(c, t):
             nc.vector.tensor_copy(own[c][:, t, :], h[t][:].indirect(entries(cen_sb, *CHUNKS[c])))
 
-        def max_first(u):
-            nc.vector.tensor_tensor(z[:, 2 * u : 2 * u + 2, :], nbr[0][:, 2 * u : 2 * u + 2, :], nbr[1][:, 2 * u : 2 * u + 2, :], MAX)
+        def max_first(u, lo, hi):
+            rows = slice(2 * u, 2 * u + 2)
+            nc.vector.tensor_tensor(z[:, rows, lo:hi], nbr[0][:, rows, lo:hi], nbr[1][:, rows, lo:hi], MAX)
 
-        def max_last(u):
-            nc.vector.tensor_tensor(z[:, 2 * u : 2 * u + 2, :], z[:, 2 * u : 2 * u + 2, :], nbr[2][:, 2 * u : 2 * u + 2, :], MAX)
+        def max_last(u, lo, hi):
+            rows = slice(2 * u, 2 * u + 2)
+            nc.vector.tensor_tensor(z[:, rows, lo:hi], z[:, rows, lo:hi], nbr[2][:, rows, lo:hi], MAX)
 
+        half = V // 2
         for t in (0, 1):
             for d in range(3):
-                fetch_nbr(d, t)
-        fetch_nbr(0, 2)
-        max_first(0)
-        fetch_nbr(1, 2)
-        max_last(0)
-        fetch_nbr(2, 2)
+                fetch_nbr(d, t, 0, V)
+        fetch_nbr(0, 2, 0, V)
+        max_first(0, 0, V)
+        fetch_nbr(1, 2, 0, V)
+        max_last(0, 0, V)
+        fetch_nbr(2, 2, 0, V)
         for d in range(3):
-            fetch_nbr(d, 3)
-        max_first(1)
+            fetch_nbr(d, 3, 0, half)
+        max_first(1, 0, half)
+        fetch_nbr(0, 3, half, V)
+        max_last(1, 0, half)
+        z_grouped = [interleave("z0", z[:, :, 0:half], half)]
+        fetch_nbr(1, 3, half, V)
+        fetch_nbr(2, 3, half, V)
+        max_first(1, half, V)
         fetch_own(0, 0)
-        max_last(1)
-        z_grouped = interleave("z", z, V)
+        max_last(1, half, V)
+        z_grouped.append(interleave("z1", z[:, :, half:V], half))
         for t in range(1, PACK):
             fetch_own(0, t)
-        own_grouped = [interleave("own0", own[0], 256)]
+        own_grouped = [interleave("own0", own[0][:], 256)]
         for c in range(1, len(CHUNKS)):
             for t in range(PACK):
                 fetch_own(c, t)
-            own_grouped.append(interleave("own%d" % c, own[c], 128))
-        z_codes, z_plane = quantize("z", z_grouped, V)
+            own_grouped.append(interleave("own%d" % c, own[c][:], 128))
 
-        (w3_codes, w3_plane), (w2_codes, w2_plane) = tail_weights
         for c, (lo, hi) in enumerate(CHUNKS):
+            if lo % half == 0:
+                z_codes, z_plane = quantize("z%d" % (lo // half), z_grouped[lo // half], half)
+            z_cols = slice(lo % half, lo % half + hi - lo)
             own_codes, own_plane = quantize("own%d" % c, own_grouped[c], hi - lo)
             acc = psum_out.tile([P, hi - lo], F32, name="out_acc%d" % c)
             nc.tensor.matmul_mx(
-                acc[:], lhsT=w3_codes[:].bitcast(FP8X4), lhsT_scale=w3_plane[:],
-                rhs=z_codes[:, lo:hi].bitcast(FP8X4), rhs_scale=z_plane[:, lo:hi], start=True, stop=False,
+                acc[:], lhsT=tail_codes[:, 0, :].bitcast(FP8X4), lhsT_scale=tail_planes[:, 0, :],
+                rhs=z_codes[:, z_cols].bitcast(FP8X4), rhs_scale=z_plane[:, z_cols], start=True, stop=False,
             )
             nc.tensor.matmul_mx(
-                acc[:], lhsT=w2_codes[:].bitcast(FP8X4), lhsT_scale=w2_plane[:],
+                acc[:], lhsT=tail_codes[:, 1, :].bitcast(FP8X4), lhsT_scale=tail_planes[:, 1, :],
                 rhs=own_codes[:].bitcast(FP8X4), rhs_scale=own_plane[:], start=False, stop=True,
             )
             result = keep.tile([P, hi - lo], F32, name="result%d" % c)

@@ -42,16 +42,16 @@ def tile_picked_sagecat_max_p_kernel(
             return tile[:, lo // LIST_ROWS : hi // LIST_ROWS]
 
         scale_table = keep.tile([P, T], U8, name="scale_table")
-        nc.sync.dma_start(scale_table[P - 16 : P, :].bitcast(I32), x_scales[0].bitcast(I32))
+        nc.scalar.dma_start(scale_table[P - 16 : P, :].bitcast(I32), x_scales[0].bitcast(I32))
         nc.vector.memset(scale_table[0 : P - 16, :].bitcast(I32), 0)
         offs_sb = load_list("offs_sb", offs)
         pos_sb = [load_list("pos%d_sb" % d, source) for d, source in enumerate((pos1, pos2))]
         x_table = keep.tile([P, T], U32, name="x_table")
         nc.sync.dma_start(x_table[:].bitcast(I32), x_words[0].rearrange("p n j -> p (n j)").bitcast(I32))
-        pos_sb.append(load_list("pos2_sb", pos3))
-        cen_sb = load_list("cen_sb", cen)
         w1_raw = keep.tile([P, PACK, H], F32, name="w1_raw", tag="raw", align_bytes=64)
         nc.sync.dma_start(w1_raw[:], w1.rearrange("(p j) c -> p j c", j=PACK))
+        pos_sb.append(load_list("pos2_sb", pos3))
+        cen_sb = load_list("cen_sb", cen)
 
         x_plane = keep.tile([P, S], U8, name="x_plane", align_bytes=64)
         nc.gpsimd.memset(x_plane[:].bitcast(I32), 0)

@@ -13,6 +13,8 @@ U16 = mybir.dt.uint16
 U8 = mybir.dt.uint8
 FP8X4 = mybir.dt.float8_e4m3fn_x4
 MAX = mybir.AluOpType.max
+SUB = mybir.AluOpType.subtract
+ADD = mybir.AluOpType.add
 COPY = mybir.ActivationFunctionType.Copy
 RELU = mybir.ActivationFunctionType.Relu
 
@@ -122,33 +124,41 @@ def tile_picked_sagecat_max_p_kernel(
             nc.vector.quantize_mx(codes[:].bitcast(FP8X4), plane[:], grouped[:].rearrange("p v t -> p (v t)"))
             return codes, plane
 
-        nbr = [keep.tile([P, PACK, V], BF16, name="nbr%d" % d) for d in range(3)]
+        nbr = [[keep.tile([P, V], BF16, name="nbr%d_%d" % (d, t)) for t in range(2)] for d in range(3)]
+        late = [keep.tile([P, 2, V], BF16, name="late%d" % d) for d in range(3)]
         z = keep.tile([P, PACK, V], BF16, name="z")
-        own = [keep.tile([P, PACK, hi - lo], BF16, name="own%d" % c) for c, (lo, hi) in enumerate(CHUNKS)]
+
+        def larger(dst, a, b, name):
+            diff = keep.tile([P, V], F32, name="diff" + name, tag="diff", bufs=2)
+            nc.gpsimd.tensor_tensor(diff[:], b, a, SUB)
+            gain = keep.tile([P, V], F32, name="gain" + name, tag="gain" + name)
+            nc.scalar.activation(gain[:], diff[:], RELU)
+            nc.gpsimd.tensor_tensor(dst, a, gain[:], ADD)
 
         def fetch_nbr(d, t, lo, hi):
-            nc.vector.tensor_copy(nbr[d][:, t, lo:hi], h[t][:].indirect(entries(pos_sb[d], lo, hi)))
+            nc.vector.tensor_copy(late[d][:, t - 2, lo:hi], h[t][:].indirect(entries(pos_sb[d], lo, hi)))
 
         def fetch_own(c, t):
             nc.vector.tensor_copy(own[c][:, t, :], h[t][:].indirect(entries(cen_sb, *CHUNKS[c])))
 
         def max_first(u, lo, hi):
-            rows = slice(2 * u, 2 * u + 2)
-            nc.vector.tensor_tensor(z[:, rows, lo:hi], nbr[0][:, rows, lo:hi], nbr[1][:, rows, lo:hi], MAX)
+            nc.vector.tensor_tensor(z[:, 2:4, lo:hi], late[0][:, :, lo:hi], late[1][:, :, lo:hi], MAX)
 
         def max_last(u, lo, hi):
-            rows = slice(2 * u, 2 * u + 2)
-            nc.vector.tensor_tensor(z[:, rows, lo:hi], z[:, rows, lo:hi], nbr[2][:, rows, lo:hi], MAX)
+            nc.vector.tensor_tensor(z[:, 2:4, lo:hi], z[:, 2:4, lo:hi], late[2][:, :, lo:hi], MAX)
 
         half = V // 2
         for t in (0, 1):
             for d in range(3):
-                fetch_nbr(d, t, 0, V)
-        fetch_nbr(0, 2, 0, V)
-        max_first(0, 0, V)
-        fetch_nbr(1, 2, 0, V)
-        max_last(0, 0, V)
-        fetch_nbr(2, 2, 0, V)
+                nc.vector.tensor_copy(nbr[d][t][:], h[t][:].indirect(pos_sb[d][:]))
+            two = keep.tile([P, V], BF16, name="two%d" % t, tag="two%d" % t)
+            larger(two[:], nbr[0][t][:], nbr[1][t][:], "a%d" % t)
+            larger(z[:, t, :], two[:], nbr[2][t][:], "b%d" % t)
+        own_first = keep.tile([P, PACK, 256], BF16, name="own_first", tag="gainb1")
+        own_rest = keep.tile([P, 2, PACK, 128], BF16, name="own_rest", tag="two1")
+        own = [own_first[:], own_rest[:, 0], own_rest[:, 1]]
+        for d in range(3):
+            fetch_nbr(d, 2, 0, V)
         for d in range(3):
             fetch_nbr(d, 3, 0, half)
         max_first(1, 0, half)
@@ -163,11 +173,11 @@ def tile_picked_sagecat_max_p_kernel(
         z_grouped.append(interleave("z1", z[:, :, half:V], half))
         for t in range(1, PACK):
             fetch_own(0, t)
-        own_grouped = [interleave("own0", own[0][:], 256)]
+        own_grouped = [interleave("own0", own[0], 256)]
         for c in range(1, len(CHUNKS)):
             for t in range(PACK):
                 fetch_own(c, t)
-            own_grouped.append(interleave("own%d" % c, own[c][:], 128))
+            own_grouped.append(interleave("own%d" % c, own[c], 128))
 
         for c, (lo, hi) in enumerate(CHUNKS):
             if lo % half == 0:

@@ -44,14 +44,16 @@ def tile_picked_sagecat_max_p_kernel(
             return tile[:, lo // LIST_ROWS : hi // LIST_ROWS]
 
         scale_table = keep.tile([P, T], U8, name="scale_table")
-        nc.scalar.dma_start(scale_table[P - 16 : P, :].bitcast(I32), x_scales[0].bitcast(I32))
-        nc.vector.memset(scale_table[0 : P - 16, :].bitcast(I32), 0)
+        nc.gpsimd.memset(scale_table[:, 0 : T // 2].bitcast(I32), 0)
+        nc.vector.memset(scale_table[:, T // 2 : T].bitcast(I32), 0)
         offs_sb = load_list("offs_sb", offs)
-        pos_sb = [load_list("pos%d_sb" % d, source) for d, source in enumerate((pos1, pos2))]
-        x_table = keep.tile([P, T], U32, name="x_table")
-        nc.sync.dma_start(x_table[:].bitcast(I32), x_words[0].rearrange("p n j -> p (n j)").bitcast(I32))
         w1_raw = keep.tile([P, PACK, H], F32, name="w1_raw", tag="raw", align_bytes=64)
         nc.sync.dma_start(w1_raw[:], w1.rearrange("(p j) c -> p j c", j=PACK))
+        nc.sync.dma_start(scale_table[32:96:4, :].bitcast(I32), x_scales[0].bitcast(I32))
+        pos_sb = [load_list("pos%d_sb" % d, source) for d, source in enumerate((pos1,))]
+        x_table = keep.tile([P, T], U32, name="x_table")
+        nc.sync.dma_start(x_table[:].bitcast(I32), x_words[0].rearrange("p n j -> p (n j)").bitcast(I32))
+        pos_sb.append(load_list("pos1_sb", pos2))
         pos_sb.append(load_list("pos2_sb", pos3))
         cen_sb = load_list("cen_sb", cen)
 
@@ -62,24 +64,27 @@ def tile_picked_sagecat_max_p_kernel(
         nc.vector.tensor_copy(picked_scales[:], scale_table[:].indirect(offs_sb[:]))
         for q in range(QUADS):
             nc.scalar.dma_start(
-                x_plane[32 * q : 32 * q + 4, :].bitcast(I32), picked_scales[P - 16 + 4 * q : P - 12 + 4 * q, :].bitcast(I32)
+                x_plane[32 * q : 32 * q + 4, :].bitcast(I32),
+                picked_scales[32 + 16 * q : 48 + 16 * q : 4, :].bitcast(I32),
             )
+
+        w1_view = w1_raw[:].rearrange("p j (m t) -> p m t j", t=PACK)
+        w1_dealt = [keep.tile([P, 2, P, PACK], BF16, name="w1_dealt%d" % u, tag="dealt%d" % u, align_bytes=64) for u in range(2)]
+        w1_codes = keep.tile([P, PACK * P], U32, name="w1_codes", align_bytes=64)
+        w1_plane = keep.tile([P, PACK * P], U8, name="w1_plane", align_bytes=64)
+        nc.vector.tensor_copy(w1_dealt[0][:].rearrange("p t m j -> p m t j"), w1_view[:, :, 0:2, :])
+        nc.scalar.activation(w1_dealt[1][:].rearrange("p t m j -> p m t j"), w1_view[:, :, 2:4, :], COPY)
+        for u in range(2):
+            cols = slice(2 * P * u, 2 * P * (u + 1))
+            nc.vector.quantize_mx(
+                w1_codes[:, cols].bitcast(FP8X4), w1_plane[:, cols], w1_dealt[u][:].rearrange("p t m j -> p (t m j)")
+            )
+
         x_codes = []
         for half in range(S // BANK):
             codes = keep.tile([P, BANK], U32, name="x_codes%d" % half, align_bytes=64)
             nc.vector.tensor_copy(codes[:], x_table[:].indirect(entries(offs_sb, half * BANK, (half + 1) * BANK)))
             x_codes.append(codes)
-
-        w1_view = w1_raw[:].rearrange("p j (m t) -> p m t j", t=PACK)
-        w1_dealt = [keep.tile([P, 2, P, PACK], BF16, name="w1_dealt%d" % u, tag="dealt%d" % u, align_bytes=64) for u in range(2)]
-        nc.vector.tensor_copy(w1_dealt[0][:].rearrange("p t m j -> p m t j"), w1_view[:, :, 0:2, :])
-        nc.scalar.activation(w1_dealt[1][:].rearrange("p t m j -> p m t j"), w1_view[:, :, 2:4, :], COPY)
-        w1_codes = [keep.tile([P, P], U32, name="w1_codes%d" % t, align_bytes=64) for t in range(PACK)]
-        w1_planes = [keep.tile([P, P], U8, name="w1_plane%d" % t, align_bytes=64) for t in range(PACK)]
-        for t in range(PACK):
-            nc.vector.quantize_mx(
-                w1_codes[t][:].bitcast(FP8X4), w1_planes[t][:], w1_dealt[t // 2][:, t % 2].rearrange("p m j -> p (m j)")
-            )
 
         tail_codes = keep.tile([P, 2, N], U32, name="tail_codes", tag="raw", align_bytes=64)
         tail_planes = keep.tile([P, 2, N], U8, name="tail_planes", tag="dealt0", align_bytes=64)
@@ -94,96 +99,75 @@ def tile_picked_sagecat_max_p_kernel(
         h = [keep.tile([P, S], F32, name="h%d" % t) for t in range(PACK)]
         for t in range(PACK):
             lo = 0
-            for piece, width in enumerate((256, 256, 256, 128, 128) if t == 0 else (BANK, BANK)):
+            for piece, width in enumerate((BANK, 256, 256) if t == 0 else (BANK, BANK)):
                 acc = psum_h.tile([P, width], F32, name="acc")
                 nc.tensor.matmul_mx(
                     acc[:],
-                    lhsT=w1_codes[t][:].bitcast(FP8X4),
-                    lhsT_scale=w1_planes[t][:],
+                    lhsT=w1_codes[:, t * P : (t + 1) * P].bitcast(FP8X4),
+                    lhsT_scale=w1_plane[:, t * P : (t + 1) * P],
                     rhs=x_codes[lo // BANK][:, lo % BANK : lo % BANK + width].bitcast(FP8X4),
                     rhs_scale=x_plane[:, lo : lo + width],
                     start=True,
                     stop=True,
                 )
-                if t == 0 and piece % 2 == 1:
+                if t == 0 and piece == 1:
                     nc.vector.tensor_scalar_max(h[t][:, lo : lo + width], acc[:], 0.0)
                 else:
                     nc.scalar.activation(h[t][:, lo : lo + width], acc[:], RELU)
                 lo = lo + width
 
-        def interleave(name, planes, width):
-            grouped = keep.tile([P, width, PACK], BF16, name=name + "_grouped", align_bytes=64)
+        def interleave(grouped, rows):
             nc.scalar.copy(
-                grouped[:].rearrange("p (c i) t -> p c t i", i=4), planes.rearrange("p t (c i) -> p c t i", i=4)
+                grouped.rearrange("p (c i) t -> p c t i", i=4), rows.rearrange("p t (c i) -> p c t i", i=4)
             )
-            return grouped
 
         def quantize(name, grouped, width):
             codes = keep.tile([P, width], U32, name=name + "_codes", align_bytes=64)
             plane = keep.tile([P, width], U8, name=name + "_plane", align_bytes=64)
-            nc.vector.quantize_mx(codes[:].bitcast(FP8X4), plane[:], grouped[:].rearrange("p v t -> p (v t)"))
+            nc.vector.quantize_mx(codes[:].bitcast(FP8X4), plane[:], grouped.rearrange("p v t -> p (v t)"))
             return codes, plane
 
-        nbr = [[keep.tile([P, V], BF16, name="nbr%d_%d" % (d, t)) for t in range(2)] for d in range(3)]
-        late = [keep.tile([P, 2, V], BF16, name="late%d" % d) for d in range(3)]
         z = keep.tile([P, PACK, V], BF16, name="z")
+        planes = keep.tile([P, 2 * PACK, V], BF16, name="planes")
+        second = planes[:, 0:PACK, :]
+        own = planes[:, PACK : 2 * PACK, :]
 
-        def larger(dst, a, b, name):
-            diff = keep.tile([P, V], F32, name="diff" + name, tag="diff", bufs=2)
+        def larger(dst, a, b, t):
+            diff = keep.tile([P, V], F32, name="diff%d" % t, tag="diff", bufs=2)
             nc.gpsimd.tensor_tensor(diff[:], b, a, SUB)
-            gain = keep.tile([P, V], F32, name="gain" + name, tag="gain" + name)
+            gain = keep.tile([P, V], F32, name="gain%d" % t)
             nc.scalar.activation(gain[:], diff[:], RELU)
             nc.gpsimd.tensor_tensor(dst, a, gain[:], ADD)
 
-        def fetch_nbr(d, t, lo, hi):
-            nc.vector.tensor_copy(late[d][:, t - 2, lo:hi], h[t][:].indirect(entries(pos_sb[d], lo, hi)))
+        def fetch(dst, t, lst, lo, hi):
+            nc.vector.tensor_copy(dst, h[t][:].indirect(entries(lst, lo, hi)))
 
-        def fetch_own(c, t):
-            nc.vector.tensor_copy(own[c][:, t, :], h[t][:].indirect(entries(cen_sb, *CHUNKS[c])))
-
-        def max_first(u, lo, hi):
-            nc.vector.tensor_tensor(z[:, 2:4, lo:hi], late[0][:, :, lo:hi], late[1][:, :, lo:hi], MAX)
-
-        def max_last(u, lo, hi):
-            nc.vector.tensor_tensor(z[:, 2:4, lo:hi], z[:, 2:4, lo:hi], late[2][:, :, lo:hi], MAX)
-
-        half = V // 2
-        for t in (0, 1):
-            for d in range(3):
-                nc.vector.tensor_copy(nbr[d][t][:], h[t][:].indirect(pos_sb[d][:]))
-            two = keep.tile([P, V], BF16, name="two%d" % t, tag="two%d" % t)
-            larger(two[:], nbr[0][t][:], nbr[1][t][:], "a%d" % t)
-            larger(z[:, t, :], two[:], nbr[2][t][:], "b%d" % t)
-        own_first = keep.tile([P, PACK, 256], BF16, name="own_first", tag="gainb1")
-        own_rest = keep.tile([P, 2, PACK, 128], BF16, name="own_rest", tag="two1")
-        own = [own_first[:], own_rest[:, 0], own_rest[:, 1]]
-        for d in range(3):
-            fetch_nbr(d, 2, 0, V)
-        for d in range(3):
-            fetch_nbr(d, 3, 0, half)
-        max_first(1, 0, half)
-        fetch_nbr(0, 3, half, V)
-        max_last(1, 0, half)
-        z_grouped = [interleave("z0", z[:, :, 0:half], half)]
-        fetch_nbr(1, 3, half, V)
-        fetch_nbr(2, 3, half, V)
-        max_first(1, half, V)
-        fetch_own(0, 0)
-        max_last(1, half, V)
-        z_grouped.append(interleave("z1", z[:, :, half:V], half))
-        for t in range(1, PACK):
-            fetch_own(0, t)
-        own_grouped = [interleave("own0", own[0], 256)]
-        for c in range(1, len(CHUNKS)):
-            for t in range(PACK):
-                fetch_own(c, t)
-            own_grouped.append(interleave("own%d" % c, own[c], 128))
+        for t in range(PACK):
+            fetch(own[:, t, :], t, pos_sb[0], 0, V)
+            fetch(second[:, t, :], t, pos_sb[1], 0, V)
+            if t < 2:
+                larger(z[:, t, :], own[:, t, :], second[:, t, :], t)
+            else:
+                larger(z[:, t, :], second[:, t, :], own[:, t, :], t)
+        for t in range(PACK):
+            fetch(own[:, t, :], t, pos_sb[2], 0, V)
+        centre = [planes[:, 2:6, 0:256]] + [own[:, :, lo:hi] for lo, hi in CHUNKS[1:]]
+        fetch(centre[0][:, 0, :], 0, cen_sb, *CHUNKS[0])
+        nc.vector.tensor_tensor(z[:], z[:], own, MAX)
+        z_grouped = keep.tile([P, V, PACK], BF16, name="z_grouped", align_bytes=64)
+        own_grouped = keep.tile([P, V, PACK], BF16, name="own_grouped", align_bytes=64)
+        for lo in range(0, V, 256):
+            interleave(z_grouped[:, lo : lo + 256, :], z[:, :, lo : lo + 256])
+        for c, (lo, hi) in enumerate(CHUNKS):
+            for t in range(1 if c == 0 else 0, PACK):
+                fetch(centre[c][:, t, :], t, cen_sb, lo, hi)
+            interleave(own_grouped[:, lo:hi, :], centre[c])
 
         for c, (lo, hi) in enumerate(CHUNKS):
-            if lo % half == 0:
-                z_codes, z_plane = quantize("z%d" % (lo // half), z_grouped[lo // half], half)
-            z_cols = slice(lo % half, lo % half + hi - lo)
-            own_codes, own_plane = quantize("own%d" % c, own_grouped[c], hi - lo)
+            if lo % 256 == 0:
+                z_codes, z_plane = quantize("z%d" % c, z_grouped[:, lo : lo + 256, :], 256)
+            z_cols = slice(lo % 256, lo % 256 + hi - lo)
+            own_codes, own_plane = quantize("own%d" % c, own_grouped[:, lo:hi, :], hi - lo)
             acc = psum_out.tile([P, hi - lo], F32, name="out_acc%d" % c)
             nc.tensor.matmul_mx(
                 acc[:], lhsT=tail_codes[:, 0, :].bitcast(FP8X4), lhsT_scale=tail_planes[:, 0, :],

@@ -23,6 +23,7 @@ PACK = 4
 QUADS = 4
 LIST_ROWS = 16
 BANK = 512
+X_HEAD = 1024
 CHUNKS = ((0, 256), (256, 384), (384, 512))
 
 
@@ -47,12 +48,14 @@ def tile_picked_sagecat_max_p_kernel(
         nc.gpsimd.memset(scale_table[:, 0 : T // 2].bitcast(I32), 0)
         nc.vector.memset(scale_table[:, T // 2 : T].bitcast(I32), 0)
         offs_sb = load_list("offs_sb", offs)
+        x_rows = x_words[0].rearrange("p n j -> p (n j)").bitcast(I32)
+        x_table = keep.tile([P, T], U32, name="x_table")
+        nc.sync.dma_start(x_table[:, 0:X_HEAD].bitcast(I32), x_rows[:, 0:X_HEAD])
+        nc.sync.dma_start(scale_table[32:96:4, :].bitcast(I32), x_scales[0].bitcast(I32))
+        pos_sb = [load_list("pos0_sb", pos1)]
+        nc.sync.dma_start(x_table[:, X_HEAD:T].bitcast(I32), x_rows[:, X_HEAD:T])
         w1_raw = keep.tile([P, PACK, H], F32, name="w1_raw", tag="raw", align_bytes=64)
         nc.sync.dma_start(w1_raw[:], w1.rearrange("(p j) c -> p j c", j=PACK))
-        nc.sync.dma_start(scale_table[32:96:4, :].bitcast(I32), x_scales[0].bitcast(I32))
-        pos_sb = [load_list("pos%d_sb" % d, source) for d, source in enumerate((pos1,))]
-        x_table = keep.tile([P, T], U32, name="x_table")
-        nc.sync.dma_start(x_table[:].bitcast(I32), x_words[0].rearrange("p n j -> p (n j)").bitcast(I32))
         pos_sb.append(load_list("pos1_sb", pos2))
         pos_sb.append(load_list("pos2_sb", pos3))
         cen_sb = load_list("cen_sb", cen)
@@ -68,23 +71,31 @@ def tile_picked_sagecat_max_p_kernel(
                 picked_scales[32 + 16 * q : 48 + 16 * q : 4, :].bitcast(I32),
             )
 
-        w1_view = w1_raw[:].rearrange("p j (m t) -> p m t j", t=PACK)
-        w1_dealt = [keep.tile([P, 2, P, PACK], BF16, name="w1_dealt%d" % u, tag="dealt%d" % u, align_bytes=64) for u in range(2)]
-        w1_codes = keep.tile([P, PACK * P], U32, name="w1_codes", align_bytes=64)
-        w1_plane = keep.tile([P, PACK * P], U8, name="w1_plane", align_bytes=64)
-        nc.vector.tensor_copy(w1_dealt[0][:].rearrange("p t m j -> p m t j"), w1_view[:, :, 0:2, :])
-        nc.scalar.activation(w1_dealt[1][:].rearrange("p t m j -> p m t j"), w1_view[:, :, 2:4, :], COPY)
-        for u in range(2):
-            cols = slice(2 * P * u, 2 * P * (u + 1))
-            nc.vector.quantize_mx(
-                w1_codes[:, cols].bitcast(FP8X4), w1_plane[:, cols], w1_dealt[u][:].rearrange("p t m j -> p (t m j)")
-            )
-
         x_codes = []
         for half in range(S // BANK):
             codes = keep.tile([P, BANK], U32, name="x_codes%d" % half, align_bytes=64)
             nc.vector.tensor_copy(codes[:], x_table[:].indirect(entries(offs_sb, half * BANK, (half + 1) * BANK)))
             x_codes.append(codes)
+
+        w1_view = w1_raw[:].rearrange("p j (m t) -> p m t j", t=PACK)
+        w1_dealt = keep.tile([P, PACK, P, PACK], BF16, name="w1_dealt", tag="dealt0", align_bytes=64)
+        dealt_view = w1_dealt[:].rearrange("p t m j -> p m t j")
+        w1_codes = keep.tile([P, PACK * P], U32, name="w1_codes", align_bytes=64)
+        w1_plane = keep.tile([P, PACK * P], U8, name="w1_plane", align_bytes=64)
+
+        def quantize_w1(t):
+            cols = slice(t * P, (t + 1) * P)
+            nc.vector.quantize_mx(
+                w1_codes[:, cols].bitcast(FP8X4), w1_plane[:, cols], w1_dealt[:, t].rearrange("p m j -> p (m j)")
+            )
+
+        nc.vector.tensor_copy(dealt_view[:, 0 : P // 2, 0:1, :], w1_view[:, 0 : P // 2, 0:1, :])
+        nc.scalar.activation(dealt_view[:, P // 2 : P, 0:1, :], w1_view[:, P // 2 : P, 0:1, :], COPY)
+        quantize_w1(0)
+        nc.scalar.activation(dealt_view[:, :, 1:3, :], w1_view[:, :, 1:3, :], COPY)
+        nc.vector.tensor_copy(dealt_view[:, :, 3:4, :], w1_view[:, :, 3:4, :])
+        for t in range(1, PACK):
+            quantize_w1(t)
 
         tail_codes = keep.tile([P, 2, N], U32, name="tail_codes", tag="raw", align_bytes=64)
         tail_planes = keep.tile([P, 2, N], U8, name="tail_planes", tag="dealt0", align_bytes=64)
@@ -99,7 +110,7 @@ def tile_picked_sagecat_max_p_kernel(
         h = [keep.tile([P, S], F32, name="h%d" % t) for t in range(PACK)]
         for t in range(PACK):
             lo = 0
-            for piece, width in enumerate((BANK, 256, 256) if t == 0 else (BANK, BANK)):
+            for piece, width in enumerate((256, 256, 256, 256) if t == 0 else (BANK, BANK)):
                 acc = psum_h.tile([P, width], F32, name="acc")
                 nc.tensor.matmul_mx(
                     acc[:],
@@ -110,7 +121,7 @@ def tile_picked_sagecat_max_p_kernel(
                     start=True,
                     stop=True,
                 )
-                if t == 0 and piece == 1:
+                if t == 0 and piece % 2 == 0:
                     nc.vector.tensor_scalar_max(h[t][:, lo : lo + width], acc[:], 0.0)
                 else:
                     nc.scalar.activation(h[t][:, lo : lo + width], acc[:], RELU)
@@ -178,5 +189,8 @@ def tile_picked_sagecat_max_p_kernel(
                 rhs=own_codes[:].bitcast(FP8X4), rhs_scale=own_plane[:], start=False, stop=True,
             )
             result = keep.tile([P, hi - lo], F32, name="result%d" % c)
-            nc.scalar.copy(result[:], acc[:])
+            if hi == V:
+                nc.vector.tensor_copy(result[:], acc[:])
+            else:
+                nc.scalar.copy(result[:], acc[:])
             nc.sync.dma_start(out[:, lo:hi], result[:])

@@ -15,6 +15,7 @@ FP8X4 = mybir.dt.float8_e4m3fn_x4
 MAX = mybir.AluOpType.max
 SUB = mybir.AluOpType.subtract
 ADD = mybir.AluOpType.add
+MULT = mybir.AluOpType.mult
 COPY = mybir.ActivationFunctionType.Copy
 RELU = mybir.ActivationFunctionType.Relu
 
@@ -47,16 +48,20 @@ def tile_picked_sagecat_max_p_kernel(
         scale_table = keep.tile([P, T], U8, name="scale_table")
         nc.gpsimd.memset(scale_table[:, 0 : T // 2].bitcast(I32), 0)
         nc.vector.memset(scale_table[:, T // 2 : T].bitcast(I32), 0)
-        offs_sb = load_list("offs_sb", offs)
+        idle = keep.tile([P, 16], F32, name="idle")
+        nc.gpsimd.memset(idle[:, 0:8], 0.0)
+        nc.scalar.activation(idle[:, 8:9], idle[:, 0:1], RELU)
         x_rows = x_words[0].rearrange("p n j -> p (n j)").bitcast(I32)
         x_table = keep.tile([P, T], U32, name="x_table")
         nc.sync.dma_start(x_table[:, 0:X_HEAD].bitcast(I32), x_rows[:, 0:X_HEAD])
+        offs_sb = load_list("offs_sb", offs)
         nc.sync.dma_start(scale_table[32:96:4, :].bitcast(I32), x_scales[0].bitcast(I32))
-        pos_sb = [load_list("pos0_sb", pos1)]
+        pos_sb = [load_list("pos0_sb", pos1), load_list("pos1_sb", pos2)]
         nc.sync.dma_start(x_table[:, X_HEAD:T].bitcast(I32), x_rows[:, X_HEAD:T])
-        w1_raw = keep.tile([P, PACK, H], F32, name="w1_raw", tag="raw", align_bytes=64)
-        nc.sync.dma_start(w1_raw[:], w1.rearrange("(p j) c -> p j c", j=PACK))
-        pos_sb.append(load_list("pos1_sb", pos2))
+        w1_rows = w1.rearrange("(p j) c -> p j c", j=PACK)
+        w1_raw = [keep.tile([P, 2, H], F32, name="w1_raw%d" % u, tag="raw%d" % u, align_bytes=64) for u in range(2)]
+        for u in range(2):
+            nc.sync.dma_start(w1_raw[u][:], w1_rows[:, 2 * u : 2 * u + 2, :])
         pos_sb.append(load_list("pos2_sb", pos3))
         cen_sb = load_list("cen_sb", cen)
 
@@ -77,7 +82,7 @@ def tile_picked_sagecat_max_p_kernel(
             nc.vector.tensor_copy(codes[:], x_table[:].indirect(entries(offs_sb, half * BANK, (half + 1) * BANK)))
             x_codes.append(codes)
 
-        w1_view = w1_raw[:].rearrange("p j (m t) -> p m t j", t=PACK)
+        w1_view = [raw[:].rearrange("p j (m t) -> p m t j", t=PACK) for raw in w1_raw]
         w1_dealt = keep.tile([P, PACK, P, PACK], BF16, name="w1_dealt", tag="dealt0", align_bytes=64)
         dealt_view = w1_dealt[:].rearrange("p t m j -> p m t j")
         w1_codes = keep.tile([P, PACK * P], U32, name="w1_codes", align_bytes=64)
@@ -89,15 +94,16 @@ def tile_picked_sagecat_max_p_kernel(
                 w1_codes[:, cols].bitcast(FP8X4), w1_plane[:, cols], w1_dealt[:, t].rearrange("p m j -> p (m j)")
             )
 
-        nc.vector.tensor_copy(dealt_view[:, 0 : P // 2, 0:1, :], w1_view[:, 0 : P // 2, 0:1, :])
-        nc.scalar.activation(dealt_view[:, P // 2 : P, 0:1, :], w1_view[:, P // 2 : P, 0:1, :], COPY)
+        for u in range(2):
+            nc.scalar.activation(dealt_view[:, :, 0:1, 2 * u : 2 * u + 2], w1_view[u][:, :, 0:1, :], COPY)
         quantize_w1(0)
-        nc.scalar.activation(dealt_view[:, :, 1:3, :], w1_view[:, :, 1:3, :], COPY)
-        nc.vector.tensor_copy(dealt_view[:, :, 3:4, :], w1_view[:, :, 3:4, :])
+        for u in range(2):
+            nc.scalar.activation(dealt_view[:, :, 1:3, 2 * u : 2 * u + 2], w1_view[u][:, :, 1:3, :], COPY)
+            nc.vector.tensor_copy(dealt_view[:, :, 3:4, 2 * u : 2 * u + 2], w1_view[u][:, :, 3:4, :])
         for t in range(1, PACK):
             quantize_w1(t)
 
-        tail_codes = keep.tile([P, 2, N], U32, name="tail_codes", tag="raw", align_bytes=64)
+        tail_codes = keep.tile([P, 2, N], U32, name="tail_codes", tag="raw1", align_bytes=64)
         tail_planes = keep.tile([P, 2, N], U8, name="tail_planes", tag="dealt0", align_bytes=64)
         nc.gpsimd.memset(tail_planes[:].rearrange("p w n -> p (w n)").bitcast(I32), 0)
         for w, (words, scales) in enumerate(((w3_words, w3_scales), (w2_words, w2_scales))):
@@ -110,7 +116,7 @@ def tile_picked_sagecat_max_p_kernel(
         h = [keep.tile([P, S], F32, name="h%d" % t) for t in range(PACK)]
         for t in range(PACK):
             lo = 0
-            for piece, width in enumerate((256, 256, 256, 256) if t == 0 else (BANK, BANK)):
+            for piece, width in enumerate((256, 256, 256, 128, 128) if t == 0 else (BANK, BANK)):
                 acc = psum_h.tile([P, width], F32, name="acc")
                 nc.tensor.matmul_mx(
                     acc[:],
@@ -121,7 +127,7 @@ def tile_picked_sagecat_max_p_kernel(
                     start=True,
                     stop=True,
                 )
-                if t == 0 and piece % 2 == 0:
+                if t == 0 and piece in (0, 2):
                     nc.vector.tensor_scalar_max(h[t][:, lo : lo + width], acc[:], 0.0)
                 else:
                     nc.scalar.activation(h[t][:, lo : lo + width], acc[:], RELU)
@@ -162,35 +168,56 @@ def tile_picked_sagecat_max_p_kernel(
                 larger(z[:, t, :], second[:, t, :], own[:, t, :], t)
         for t in range(PACK):
             fetch(own[:, t, :], t, pos_sb[2], 0, V)
-        centre = [planes[:, 2:6, 0:256]] + [own[:, :, lo:hi] for lo, hi in CHUNKS[1:]]
-        fetch(centre[0][:, 0, :], 0, cen_sb, *CHUNKS[0])
-        nc.vector.tensor_tensor(z[:], z[:], own, MAX)
-        z_grouped = keep.tile([P, V, PACK], BF16, name="z_grouped", align_bytes=64)
+        half = V // 2
         own_grouped = keep.tile([P, V, PACK], BF16, name="own_grouped", align_bytes=64)
-        for lo in range(0, V, 256):
-            interleave(z_grouped[:, lo : lo + 256, :], z[:, :, lo : lo + 256])
-        for c, (lo, hi) in enumerate(CHUNKS):
-            for t in range(1 if c == 0 else 0, PACK):
-                fetch(centre[c][:, t, :], t, cen_sb, lo, hi)
-            interleave(own_grouped[:, lo:hi, :], centre[c])
+        out_acc = [psum_out.tile([P, hi - lo], F32, name="out_acc%d" % c) for c, (lo, hi) in enumerate(CHUNKS)]
+
+        def fetch_centre(c, centre, tiles):
+            lo, hi = CHUNKS[c]
+            for t in tiles:
+                fetch(centre[:, t, :], t, cen_sb, lo, hi)
+
+        def quantize_z(u):
+            codes, plane = quantize("z%d" % u, z_grouped[u][:], half)
+            for c, (lo, hi) in enumerate(CHUNKS):
+                if lo // half == u:
+                    cols = slice(lo % half, lo % half + hi - lo)
+                    nc.tensor.matmul_mx(
+                        out_acc[c][:], lhsT=tail_codes[:, 0, :].bitcast(FP8X4), lhsT_scale=tail_planes[:, 0, :],
+                        rhs=codes[:, cols].bitcast(FP8X4), rhs_scale=plane[:, cols], start=True, stop=False,
+                    )
+
+        centre = planes[:, 2:6, 0:half]
+        fetch_centre(0, centre, range(1))
+        nc.vector.tensor_tensor(z[:], z[:], own, MAX)
+        z_grouped = []
+        for u in range(2):
+            grouped = keep.tile([P, half, PACK], BF16, name="z_grouped%d" % u, tag="z_grouped%d" % u, align_bytes=64)
+            interleave(grouped[:], z[:, :, u * half : (u + 1) * half])
+            z_grouped.append(grouped)
+        fetch_centre(0, centre, range(1, PACK))
+        nc.gpsimd.tensor_scalar(own_grouped[:, 0:half, :], centre.rearrange("p t v -> p v t"), 1.0, 0.0, MULT, ADD)
+        quantize_z(0)
+        centre = z[:, :, 0:128]
+        fetch_centre(1, centre, range(PACK))
+        interleave(own_grouped[:, half : half + 128, :], centre)
+        centre = z[:, :, 128:half]
+        fetch_centre(2, centre, range(PACK - 1))
+        for lo in (0, 64):
+            fetch(centre[:, PACK - 1, lo : lo + 64], PACK - 1, cen_sb, V - 128 + lo, V - 64 + lo)
+            interleave(own_grouped[:, V - 128 + lo : V - 64 + lo, :], centre[:, :, lo : lo + 64])
 
         for c, (lo, hi) in enumerate(CHUNKS):
-            if lo % 256 == 0:
-                z_codes, z_plane = quantize("z%d" % c, z_grouped[:, lo : lo + 256, :], 256)
-            z_cols = slice(lo % 256, lo % 256 + hi - lo)
+            if c == 1:
+                quantize_z(1)
             own_codes, own_plane = quantize("own%d" % c, own_grouped[:, lo:hi, :], hi - lo)
-            acc = psum_out.tile([P, hi - lo], F32, name="out_acc%d" % c)
             nc.tensor.matmul_mx(
-                acc[:], lhsT=tail_codes[:, 0, :].bitcast(FP8X4), lhsT_scale=tail_planes[:, 0, :],
-                rhs=z_codes[:, z_cols].bitcast(FP8X4), rhs_scale=z_plane[:, z_cols], start=True, stop=False,
-            )
-            nc.tensor.matmul_mx(
-                acc[:], lhsT=tail_codes[:, 1, :].bitcast(FP8X4), lhsT_scale=tail_planes[:, 1, :],
+                out_acc[c][:], lhsT=tail_codes[:, 1, :].bitcast(FP8X4), lhsT_scale=tail_planes[:, 1, :],
                 rhs=own_codes[:].bitcast(FP8X4), rhs_scale=own_plane[:], start=False, stop=True,
             )
             result = keep.tile([P, hi - lo], F32, name="result%d" % c)
             if hi == V:
-                nc.vector.tensor_copy(result[:], acc[:])
+                nc.vector.tensor_copy(result[:], out_acc[c][:])
             else:
-                nc.scalar.copy(result[:], acc[:])
+                nc.scalar.copy(result[:], out_acc[c][:])
             nc.sync.dma_start(out[:, lo:hi], result[:])

@@ -68,7 +68,7 @@ def tile_picked_sagecat_max_p_kernel(
         x_plane = keep.tile([P, S], U8, name="x_plane", align_bytes=64)
         nc.gpsimd.memset(x_plane[:].bitcast(I32), 0)
 
-        picked_scales = keep.tile([P, S], U8, name="picked_scales")
+        picked_scales = keep.tile([P, S], U8, name="picked_scales", align_bytes=64)
         nc.vector.tensor_copy(picked_scales[:], scale_table[:].indirect(offs_sb[:]))
         for q in range(QUADS):
             nc.scalar.dma_start(
@@ -81,6 +81,13 @@ def tile_picked_sagecat_max_p_kernel(
             codes = keep.tile([P, BANK], U32, name="x_codes%d" % half, align_bytes=64)
             nc.vector.tensor_copy(codes[:], x_table[:].indirect(entries(offs_sb, half * BANK, (half + 1) * BANK)))
             x_codes.append(codes)
+
+        for n in range(2):
+            spare = psum_out.tile([P, BANK], F32, name="spare", tag="out_acc%d" % n)
+            nc.tensor.matmul_mx(
+                spare[:], lhsT=x_codes[0][:, 0:P].bitcast(FP8X4), lhsT_scale=picked_scales[:, 0:P],
+                rhs=x_codes[0][:].bitcast(FP8X4), rhs_scale=picked_scales[:, 0:BANK], start=True, stop=True,
+            )
 
         w1_view = [raw[:].rearrange("p j (m t) -> p m t j", t=PACK) for raw in w1_raw]
         w1_dealt = keep.tile([P, PACK, P, PACK], BF16, name="w1_dealt", tag="dealt0", align_bytes=64)
@@ -116,7 +123,7 @@ def tile_picked_sagecat_max_p_kernel(
         h = [keep.tile([P, S], F32, name="h%d" % t) for t in range(PACK)]
         for t in range(PACK):
             lo = 0
-            for piece, width in enumerate((256, 256, 256, 128, 128) if t == 0 else (BANK, BANK)):
+            for piece, width in enumerate((256, 256, 256, 128, 128) if t == 0 else (256, 256, 256, 256)):
                 acc = psum_h.tile([P, width], F32, name="acc")
                 nc.tensor.matmul_mx(
                     acc[:],
@@ -170,7 +177,7 @@ def tile_picked_sagecat_max_p_kernel(
             fetch(own[:, t, :], t, pos_sb[2], 0, V)
         half = V // 2
         own_grouped = keep.tile([P, V, PACK], BF16, name="own_grouped", align_bytes=64)
-        out_acc = [psum_out.tile([P, hi - lo], F32, name="out_acc%d" % c) for c, (lo, hi) in enumerate(CHUNKS)]
+        out_acc = [psum_out.tile([P, hi - lo], F32, name="out_acc%d" % c, tag="out_acc%d" % c) for c, (lo, hi) in enumerate(CHUNKS)]
 
         def fetch_centre(c, centre, tiles):
             lo, hi = CHUNKS[c]

@@ -24,7 +24,7 @@ PACK = 4
 QUADS = 4
 LIST_ROWS = 16
 BANK = 512
-X_HEAD = 1024
+X_HEAD = 1536
 CHUNKS = ((0, 256), (256, 384), (384, 512))
 
 
@@ -55,8 +55,8 @@ def tile_picked_sagecat_max_p_kernel(
         x_table = keep.tile([P, T], U32, name="x_table")
         nc.sync.dma_start(x_table[:, 0:X_HEAD].bitcast(I32), x_rows[:, 0:X_HEAD])
         offs_sb = load_list("offs_sb", offs)
-        nc.sync.dma_start(scale_table[32:96:4, :].bitcast(I32), x_scales[0].bitcast(I32))
         pos_sb = [load_list("pos0_sb", pos1), load_list("pos1_sb", pos2)]
+        nc.sync.dma_start(scale_table[32:96:4, :].bitcast(I32), x_scales[0].bitcast(I32))
         nc.sync.dma_start(x_table[:, X_HEAD:T].bitcast(I32), x_rows[:, X_HEAD:T])
         w1_rows = w1.rearrange("(p j) c -> p j c", j=PACK)
         w1_raw = [keep.tile([P, 2, H], F32, name="w1_raw%d" % u, tag="raw%d" % u, align_bytes=64) for u in range(2)]

@@ -59,9 +59,9 @@ def tile_picked_sagecat_max_p_kernel(
         nc.sync.dma_start(scale_table[32:96:4, :].bitcast(I32), x_scales[0].bitcast(I32))
         nc.sync.dma_start(x_table[:, X_HEAD:T].bitcast(I32), x_rows[:, X_HEAD:T])
         w1_rows = w1.rearrange("(p j) c -> p j c", j=PACK)
-        w1_raw = [keep.tile([P, 2, H], F32, name="w1_raw%d" % u, tag="raw%d" % u, align_bytes=64) for u in range(2)]
+        w1_raw = keep.tile([P, PACK, H], F32, name="w1_raw", tag="raw1", align_bytes=64)
         for u in range(2):
-            nc.sync.dma_start(w1_raw[u][:], w1_rows[:, 2 * u : 2 * u + 2, :])
+            nc.sync.dma_start(w1_raw[:, 2 * u : 2 * u + 2, :], w1_rows[:, 2 * u : 2 * u + 2, :])
         pos_sb.append(load_list("pos2_sb", pos3))
         cen_sb = load_list("cen_sb", cen)
 
@@ -89,41 +89,30 @@ def tile_picked_sagecat_max_p_kernel(
                 rhs=x_codes[0][:].bitcast(FP8X4), rhs_scale=picked_scales[:, 0:BANK], start=True, stop=True,
             )
 
-        w1_view = [raw[:].rearrange("p j (m t) -> p m t j", t=PACK) for raw in w1_raw]
-        w1_dealt = keep.tile([P, PACK, P, PACK], BF16, name="w1_dealt", tag="dealt0", align_bytes=64)
-        dealt_view = w1_dealt[:].rearrange("p t m j -> p m t j")
+        w1_view = w1_raw[:].rearrange("p j (m t) -> p m t j", t=PACK)
+        dealt_low = keep.tile([P, 2, P, PACK], BF16, name="dealt_low", tag="dealt0", align_bytes=64)
+        dealt_high = keep.tile([P, 2, P, PACK], BF16, name="dealt_high", align_bytes=64)
+        low_view = dealt_low[:].rearrange("p t m j -> p m t j")
         w1_codes = keep.tile([P, PACK * P], U32, name="w1_codes", align_bytes=64)
         w1_plane = keep.tile([P, PACK * P], U8, name="w1_plane", align_bytes=64)
 
-        def quantize_w1(t):
-            cols = slice(t * P, (t + 1) * P)
+        def quantize_w1(lo, hi, dealt):
             nc.vector.quantize_mx(
-                w1_codes[:, cols].bitcast(FP8X4), w1_plane[:, cols], w1_dealt[:, t].rearrange("p m j -> p (m j)")
+                w1_codes[:, lo * P : hi * P].bitcast(FP8X4), w1_plane[:, lo * P : hi * P],
+                dealt.rearrange("p t m j -> p (t m j)"),
             )
 
-        for u in range(2):
-            nc.scalar.activation(dealt_view[:, :, 0:1, 2 * u : 2 * u + 2], w1_view[u][:, :, 0:1, :], COPY)
-        quantize_w1(0)
-        for u in range(2):
-            nc.scalar.activation(dealt_view[:, :, 1:3, 2 * u : 2 * u + 2], w1_view[u][:, :, 1:3, :], COPY)
-            nc.vector.tensor_copy(dealt_view[:, :, 3:4, 2 * u : 2 * u + 2], w1_view[u][:, :, 3:4, :])
-        for t in range(1, PACK):
-            quantize_w1(t)
-
-        tail_codes = keep.tile([P, 2, N], U32, name="tail_codes", tag="raw1", align_bytes=64)
-        tail_planes = keep.tile([P, 2, N], U8, name="tail_planes", tag="dealt0", align_bytes=64)
-        nc.gpsimd.memset(tail_planes[:].rearrange("p w n -> p (w n)").bitcast(I32), 0)
-        for w, (words, scales) in enumerate(((w3_words, w3_scales), (w2_words, w2_scales))):
-            nc.sync.dma_start(tail_codes[:, w, :].bitcast(I32), words[0].rearrange("p n j -> p (n j)").bitcast(I32))
-            for q in range(QUADS):
-                nc.sync.dma_start(
-                    tail_planes[32 * q : 32 * q + 4, w, :].bitcast(I32), scales[0, 4 * q : 4 * q + 4, :].bitcast(I32)
-                )
+        nc.scalar.activation(low_view[:, :, :, 0:2], w1_view[:, :, 0:PACK:3, 0:2], COPY)
+        for t in range(2):
+            nc.scalar.activation(low_view[:, :, t, 2:4], w1_view[:, :, 3 * t, 2:4], COPY)
+        nc.vector.tensor_copy(dealt_high[:].rearrange("p t m j -> p m t j"), w1_view[:, :, 1:3, :])
+        quantize_w1(0, 1, dealt_low[:, 0:1])
+        quantize_w1(1, 3, dealt_high[:])
 
         h = [keep.tile([P, S], F32, name="h%d" % t) for t in range(PACK)]
         for t in range(PACK):
             lo = 0
-            for piece, width in enumerate((256, 256, 256, 128, 128) if t == 0 else (256, 256, 256, 256)):
+            for piece, width in enumerate((256, 256, 256, 256)):
                 acc = psum_h.tile([P, width], F32, name="acc")
                 nc.tensor.matmul_mx(
                     acc[:],
@@ -138,7 +127,19 @@ def tile_picked_sagecat_max_p_kernel(
                     nc.vector.tensor_scalar_max(h[t][:, lo : lo + width], acc[:], 0.0)
                 else:
                     nc.scalar.activation(h[t][:, lo : lo + width], acc[:], RELU)
+                if t == 0 and piece == 3:
+                    quantize_w1(3, 4, dealt_low[:, 1:2])
                 lo = lo + width
+
+        tail_codes = keep.tile([P, 2, N], U32, name="tail_codes", tag="raw1", align_bytes=64)
+        tail_planes = keep.tile([P, 2, N], U8, name="tail_planes", tag="dealt0", align_bytes=64)
+        nc.gpsimd.memset(tail_planes[:].rearrange("p w n -> p (w n)").bitcast(I32), 0)
+        for w, (words, scales) in enumerate(((w3_words, w3_scales), (w2_words, w2_scales))):
+            nc.sync.dma_start(tail_codes[:, w, :].bitcast(I32), words[0].rearrange("p n j -> p (n j)").bitcast(I32))
+            for q in range(QUADS):
+                nc.sync.dma_start(
+                    tail_planes[32 * q : 32 * q + 4, w, :].bitcast(I32), scales[0, 4 * q : 4 * q + 4, :].bitcast(I32)
+                )
 
         def interleave(grouped, rows):
             nc.scalar.copy(

@@ -25,7 +25,13 @@ QUADS = 4
 LIST_ROWS = 16
 BANK = 512
 X_HEAD = 1536
-CHUNKS = ((0, 256), (256, 384), (384, 512))
+FIRST_PIECES = (256, 256, 256, 128, 128)
+VECTOR_PIECES = (0, 2)
+LATER_PIECES = (256, 256, 256, 256)
+H_BANKS = 5
+HALF = V // 2
+CHUNKS = ((0, HALF), (HALF, HALF + 128), (HALF + 128, V))
+LAST_PIECE = 64
 
 
 def tile_picked_sagecat_max_p_kernel(
@@ -34,7 +40,7 @@ def tile_picked_sagecat_max_p_kernel(
     nc = tc.nc
     with ExitStack() as ctx:
         keep = ctx.enter_context(tc.tile_pool(name="keep", bufs=1))
-        psum_h = ctx.enter_context(tc.psum_pool(name="psum_h", bufs=5))
+        psum_h = ctx.enter_context(tc.psum_pool(name="psum_h", bufs=H_BANKS))
         psum_out = ctx.enter_context(tc.psum_pool(name="psum_out", bufs=1))
 
         def load_list(name, source):
@@ -51,6 +57,7 @@ def tile_picked_sagecat_max_p_kernel(
         idle = keep.tile([P, 16], F32, name="idle")
         nc.gpsimd.memset(idle[:, 0:8], 0.0)
         nc.scalar.activation(idle[:, 8:9], idle[:, 0:1], RELU)
+
         x_rows = x_words[0].rearrange("p n j -> p (n j)").bitcast(I32)
         x_table = keep.tile([P, T], U32, name="x_table")
         nc.sync.dma_start(x_table[:, 0:X_HEAD].bitcast(I32), x_rows[:, 0:X_HEAD])
@@ -59,9 +66,9 @@ def tile_picked_sagecat_max_p_kernel(
         nc.sync.dma_start(scale_table[32:96:4, :].bitcast(I32), x_scales[0].bitcast(I32))
         nc.sync.dma_start(x_table[:, X_HEAD:T].bitcast(I32), x_rows[:, X_HEAD:T])
         w1_rows = w1.rearrange("(p j) c -> p j c", j=PACK)
-        w1_raw = keep.tile([P, PACK, H], F32, name="w1_raw", tag="raw1", align_bytes=64)
-        for u in range(2):
-            nc.sync.dma_start(w1_raw[:, 2 * u : 2 * u + 2, :], w1_rows[:, 2 * u : 2 * u + 2, :])
+        w1_raw = keep.tile([P, PACK, H], F32, name="w1_raw", tag="w1_raw", align_bytes=64)
+        for pair in range(2):
+            nc.sync.dma_start(w1_raw[:, 2 * pair : 2 * pair + 2, :], w1_rows[:, 2 * pair : 2 * pair + 2, :])
         pos_sb.append(load_list("pos2_sb", pos3))
         cen_sb = load_list("cen_sb", cen)
 
@@ -77,9 +84,9 @@ def tile_picked_sagecat_max_p_kernel(
             )
 
         x_codes = []
-        for half in range(S // BANK):
-            codes = keep.tile([P, BANK], U32, name="x_codes%d" % half, align_bytes=64)
-            nc.vector.tensor_copy(codes[:], x_table[:].indirect(entries(offs_sb, half * BANK, (half + 1) * BANK)))
+        for part in range(S // BANK):
+            codes = keep.tile([P, BANK], U32, name="x_codes%d" % part, align_bytes=64)
+            nc.vector.tensor_copy(codes[:], x_table[:].indirect(entries(offs_sb, part * BANK, (part + 1) * BANK)))
             x_codes.append(codes)
 
         for n in range(2):
@@ -90,29 +97,29 @@ def tile_picked_sagecat_max_p_kernel(
             )
 
         w1_view = w1_raw[:].rearrange("p j (m t) -> p m t j", t=PACK)
-        dealt_low = keep.tile([P, 2, P, PACK], BF16, name="dealt_low", tag="dealt0", align_bytes=64)
-        dealt_high = keep.tile([P, 2, P, PACK], BF16, name="dealt_high", align_bytes=64)
-        low_view = dealt_low[:].rearrange("p t m j -> p m t j")
+        dealt_outer = keep.tile([P, 2, P, PACK], BF16, name="dealt_outer", tag="dealt_outer", align_bytes=64)
+        dealt_inner = keep.tile([P, 2, P, PACK], BF16, name="dealt_inner", align_bytes=64)
+        outer_view = dealt_outer[:].rearrange("p t m j -> p m t j")
         w1_codes = keep.tile([P, PACK * P], U32, name="w1_codes", align_bytes=64)
         w1_plane = keep.tile([P, PACK * P], U8, name="w1_plane", align_bytes=64)
 
-        def quantize_w1(lo, hi, dealt):
+        def quantize_w1(first_tile, end_tile, dealt):
+            cols = slice(first_tile * P, end_tile * P)
             nc.vector.quantize_mx(
-                w1_codes[:, lo * P : hi * P].bitcast(FP8X4), w1_plane[:, lo * P : hi * P],
-                dealt.rearrange("p t m j -> p (t m j)"),
+                w1_codes[:, cols].bitcast(FP8X4), w1_plane[:, cols], dealt.rearrange("p t m j -> p (t m j)")
             )
 
-        nc.scalar.activation(low_view[:, :, :, 0:2], w1_view[:, :, 0:PACK:3, 0:2], COPY)
-        for t in range(2):
-            nc.scalar.activation(low_view[:, :, t, 2:4], w1_view[:, :, 3 * t, 2:4], COPY)
-        nc.vector.tensor_copy(dealt_high[:].rearrange("p t m j -> p m t j"), w1_view[:, :, 1:3, :])
-        quantize_w1(0, 1, dealt_low[:, 0:1])
-        quantize_w1(1, 3, dealt_high[:])
+        nc.scalar.activation(outer_view[:, :, :, 0:2], w1_view[:, :, 0:PACK:3, 0:2], COPY)
+        for place, t in enumerate((0, 3)):
+            nc.scalar.activation(outer_view[:, :, place, 2:4], w1_view[:, :, t, 2:4], COPY)
+        nc.vector.tensor_copy(dealt_inner[:].rearrange("p t m j -> p m t j"), w1_view[:, :, 1:3, :])
+        quantize_w1(0, 1, dealt_outer[:, 0:1])
+        quantize_w1(1, 3, dealt_inner[:])
 
         h = [keep.tile([P, S], F32, name="h%d" % t) for t in range(PACK)]
         for t in range(PACK):
             lo = 0
-            for piece, width in enumerate((256, 256, 256, 256)):
+            for piece, width in enumerate(FIRST_PIECES if t == 0 else LATER_PIECES):
                 acc = psum_h.tile([P, width], F32, name="acc")
                 nc.tensor.matmul_mx(
                     acc[:],
@@ -123,16 +130,16 @@ def tile_picked_sagecat_max_p_kernel(
                     start=True,
                     stop=True,
                 )
-                if t == 0 and piece in (0, 2):
+                if t == 0 and piece in VECTOR_PIECES:
                     nc.vector.tensor_scalar_max(h[t][:, lo : lo + width], acc[:], 0.0)
                 else:
                     nc.scalar.activation(h[t][:, lo : lo + width], acc[:], RELU)
-                if t == 0 and piece == 3:
-                    quantize_w1(3, 4, dealt_low[:, 1:2])
                 lo = lo + width
+            if t == 0:
+                quantize_w1(3, 4, dealt_outer[:, 1:2])
 
-        tail_codes = keep.tile([P, 2, N], U32, name="tail_codes", tag="raw1", align_bytes=64)
-        tail_planes = keep.tile([P, 2, N], U8, name="tail_planes", tag="dealt0", align_bytes=64)
+        tail_codes = keep.tile([P, 2, N], U32, name="tail_codes", tag="w1_raw", align_bytes=64)
+        tail_planes = keep.tile([P, 2, N], U8, name="tail_planes", tag="dealt_outer", align_bytes=64)
         nc.gpsimd.memset(tail_planes[:].rearrange("p w n -> p (w n)").bitcast(I32), 0)
         for w, (words, scales) in enumerate(((w3_words, w3_scales), (w2_words, w2_scales))):
             nc.sync.dma_start(tail_codes[:, w, :].bitcast(I32), words[0].rearrange("p n j -> p (n j)").bitcast(I32))
@@ -141,9 +148,9 @@ def tile_picked_sagecat_max_p_kernel(
                     tail_planes[32 * q : 32 * q + 4, w, :].bitcast(I32), scales[0, 4 * q : 4 * q + 4, :].bitcast(I32)
                 )
 
-        def interleave(grouped, rows):
+        def interleave(grouped, source):
             nc.scalar.copy(
-                grouped.rearrange("p (c i) t -> p c t i", i=4), rows.rearrange("p t (c i) -> p c t i", i=4)
+                grouped.rearrange("p (c i) t -> p c t i", i=4), source.rearrange("p t (c i) -> p c t i", i=4)
             )
 
         def quantize(name, grouped, width):
@@ -152,10 +159,8 @@ def tile_picked_sagecat_max_p_kernel(
             nc.vector.quantize_mx(codes[:].bitcast(FP8X4), plane[:], grouped.rearrange("p v t -> p (v t)"))
             return codes, plane
 
-        z = keep.tile([P, PACK, V], BF16, name="z")
-        planes = keep.tile([P, 2 * PACK, V], BF16, name="planes")
-        second = planes[:, 0:PACK, :]
-        own = planes[:, PACK : 2 * PACK, :]
+        def fetch(dst, t, lst, lo, hi):
+            nc.vector.tensor_copy(dst, h[t][:].indirect(entries(lst, lo, hi)))
 
         def larger(dst, a, b, t):
             diff = keep.tile([P, V], F32, name="diff%d" % t, tag="diff", bufs=2)
@@ -164,59 +169,67 @@ def tile_picked_sagecat_max_p_kernel(
             nc.scalar.activation(gain[:], diff[:], RELU)
             nc.gpsimd.tensor_tensor(dst, a, gain[:], ADD)
 
-        def fetch(dst, t, lst, lo, hi):
-            nc.vector.tensor_copy(dst, h[t][:].indirect(entries(lst, lo, hi)))
+        z = keep.tile([P, PACK, V], BF16, name="z")
+        rows = keep.tile([P, 2 * PACK, V], BF16, name="rows")
+        rows_b = rows[:, 0:PACK, :]
+        rows_a = rows[:, PACK : 2 * PACK, :]
 
         for t in range(PACK):
-            fetch(own[:, t, :], t, pos_sb[0], 0, V)
-            fetch(second[:, t, :], t, pos_sb[1], 0, V)
-            if t < 2:
-                larger(z[:, t, :], own[:, t, :], second[:, t, :], t)
+            fetch(rows_a[:, t, :], t, pos_sb[0], 0, V)
+            fetch(rows_b[:, t, :], t, pos_sb[1], 0, V)
+            if t < PACK // 2:
+                larger(z[:, t, :], rows_a[:, t, :], rows_b[:, t, :], t)
             else:
-                larger(z[:, t, :], second[:, t, :], own[:, t, :], t)
+                larger(z[:, t, :], rows_b[:, t, :], rows_a[:, t, :], t)
         for t in range(PACK):
-            fetch(own[:, t, :], t, pos_sb[2], 0, V)
-        half = V // 2
+            fetch(rows_a[:, t, :], t, pos_sb[2], 0, V)
         own_grouped = keep.tile([P, V, PACK], BF16, name="own_grouped", align_bytes=64)
-        out_acc = [psum_out.tile([P, hi - lo], F32, name="out_acc%d" % c, tag="out_acc%d" % c) for c, (lo, hi) in enumerate(CHUNKS)]
+        out_acc = [
+            psum_out.tile([P, hi - lo], F32, name="out_acc%d" % c, tag="out_acc%d" % c)
+            for c, (lo, hi) in enumerate(CHUNKS)
+        ]
 
-        def fetch_centre(c, centre, tiles):
+        def fetch_own(c, dst, tiles):
             lo, hi = CHUNKS[c]
             for t in tiles:
-                fetch(centre[:, t, :], t, cen_sb, lo, hi)
+                fetch(dst[:, t, :], t, cen_sb, lo, hi)
 
         def quantize_z(u):
-            codes, plane = quantize("z%d" % u, z_grouped[u][:], half)
+            codes, plane = quantize("z%d" % u, z_grouped[u][:], HALF)
             for c, (lo, hi) in enumerate(CHUNKS):
-                if lo // half == u:
-                    cols = slice(lo % half, lo % half + hi - lo)
+                if lo // HALF == u:
+                    cols = slice(lo % HALF, lo % HALF + hi - lo)
                     nc.tensor.matmul_mx(
                         out_acc[c][:], lhsT=tail_codes[:, 0, :].bitcast(FP8X4), lhsT_scale=tail_planes[:, 0, :],
                         rhs=codes[:, cols].bitcast(FP8X4), rhs_scale=plane[:, cols], start=True, stop=False,
                     )
 
-        centre = planes[:, 2:6, 0:half]
-        fetch_centre(0, centre, range(1))
-        nc.vector.tensor_tensor(z[:], z[:], own, MAX)
+        own_first = rows[:, 2:6, 0:HALF]
+        fetch_own(0, own_first, range(1))
+        nc.vector.tensor_tensor(z[:], z[:], rows_a, MAX)
         z_grouped = []
         for u in range(2):
-            grouped = keep.tile([P, half, PACK], BF16, name="z_grouped%d" % u, tag="z_grouped%d" % u, align_bytes=64)
-            interleave(grouped[:], z[:, :, u * half : (u + 1) * half])
+            grouped = keep.tile([P, HALF, PACK], BF16, name="z_grouped%d" % u, tag="z_grouped%d" % u, align_bytes=64)
+            interleave(grouped[:], z[:, :, u * HALF : (u + 1) * HALF])
             z_grouped.append(grouped)
-        fetch_centre(0, centre, range(1, PACK))
-        nc.gpsimd.tensor_scalar(own_grouped[:, 0:half, :], centre.rearrange("p t v -> p v t"), 1.0, 0.0, MULT, ADD)
+        fetch_own(0, own_first, range(1, PACK))
+        nc.gpsimd.tensor_scalar(own_grouped[:, 0:HALF, :], own_first.rearrange("p t v -> p v t"), 1.0, 0.0, MULT, ADD)
         quantize_z(0)
-        centre = z[:, :, 0:128]
-        fetch_centre(1, centre, range(PACK))
-        interleave(own_grouped[:, half : half + 128, :], centre)
-        centre = z[:, :, 128:half]
-        fetch_centre(2, centre, range(PACK - 1))
-        for lo in (0, 64):
-            fetch(centre[:, PACK - 1, lo : lo + 64], PACK - 1, cen_sb, V - 128 + lo, V - 64 + lo)
-            interleave(own_grouped[:, V - 128 + lo : V - 64 + lo, :], centre[:, :, lo : lo + 64])
+
+        lo, hi = CHUNKS[1]
+        own_second = z[:, :, lo - HALF : hi - HALF]
+        fetch_own(1, own_second, range(PACK))
+        interleave(own_grouped[:, lo:hi, :], own_second)
+        lo, hi = CHUNKS[2]
+        own_third = z[:, :, lo - HALF : hi - HALF]
+        fetch_own(2, own_third, range(PACK - 1))
+        for at in range(0, hi - lo, LAST_PIECE):
+            piece_cols = slice(at, at + LAST_PIECE)
+            fetch(own_third[:, PACK - 1, piece_cols], PACK - 1, cen_sb, lo + at, lo + at + LAST_PIECE)
+            interleave(own_grouped[:, lo + at : lo + at + LAST_PIECE, :], own_third[:, :, piece_cols])
 
         for c, (lo, hi) in enumerate(CHUNKS):
-            if c == 1:
+            if lo == HALF:
                 quantize_z(1)
             own_codes, own_plane = quantize("own%d" % c, own_grouped[:, lo:hi, :], hi - lo)
             nc.tensor.matmul_mx(

@@ -23,15 +23,11 @@ P = 128
 PACK = 4
 QUADS = 4
 LIST_ROWS = 16
-BANK = 512
-X_HEAD = 1536
-FIRST_PIECES = (256, 256, 256, 128, 128)
-VECTOR_PIECES = (0, 2)
-LATER_PIECES = (256, 256, 256, 256)
+PIECE = 256
 H_BANKS = 5
 HALF = V // 2
-CHUNKS = ((0, HALF), (HALF, HALF + 128), (HALF + 128, V))
-LAST_PIECE = 64
+QUARTER = V // 4
+CHUNKS = ((0, HALF), (HALF, HALF + QUARTER), (HALF + QUARTER, V))
 
 
 def tile_picked_sagecat_max_p_kernel(
@@ -54,102 +50,97 @@ def tile_picked_sagecat_max_p_kernel(
         scale_table = keep.tile([P, T], U8, name="scale_table")
         nc.gpsimd.memset(scale_table[:, 0 : T // 2].bitcast(I32), 0)
         nc.vector.memset(scale_table[:, T // 2 : T].bitcast(I32), 0)
-        idle = keep.tile([P, 16], F32, name="idle")
-        nc.gpsimd.memset(idle[:, 0:8], 0.0)
-        nc.scalar.activation(idle[:, 8:9], idle[:, 0:1], RELU)
 
-        x_rows = x_words[0].rearrange("p n j -> p (n j)").bitcast(I32)
-        x_table = keep.tile([P, T], U32, name="x_table")
-        nc.sync.dma_start(x_table[:, 0:X_HEAD].bitcast(I32), x_rows[:, 0:X_HEAD])
-        offs_sb = load_list("offs_sb", offs)
-        pos_sb = [load_list("pos0_sb", pos1), load_list("pos1_sb", pos2)]
-        nc.sync.dma_start(scale_table[32:96:4, :].bitcast(I32), x_scales[0].bitcast(I32))
-        nc.sync.dma_start(x_table[:, X_HEAD:T].bitcast(I32), x_rows[:, X_HEAD:T])
         w1_rows = w1.rearrange("(p j) c -> p j c", j=PACK)
         w1_raw = keep.tile([P, PACK, H], F32, name="w1_raw", tag="w1_raw", align_bytes=64)
-        for pair in range(2):
-            nc.sync.dma_start(w1_raw[:, 2 * pair : 2 * pair + 2, :], w1_rows[:, 2 * pair : 2 * pair + 2, :])
+        nc.sync.dma_start(w1_raw[:, 0:2, :], w1_rows[:, 0:2, :])
+        offs_sb = load_list("offs_sb", offs)
+        pos_sb = [load_list("pos0_sb", pos1)]
+        nc.sync.dma_start(scale_table[32:96:4, :].bitcast(I32), x_scales[0].bitcast(I32))
+        nc.sync.dma_start(w1_raw[:, 2:4, :], w1_rows[:, 2:4, :])
+        x_table = keep.tile([P, T], U32, name="x_table")
+        nc.sync.dma_start(x_table[:].bitcast(I32), x_words[0].rearrange("p n j -> p (n j)").bitcast(I32))
+        pos_sb.append(load_list("pos1_sb", pos2))
         pos_sb.append(load_list("pos2_sb", pos3))
         cen_sb = load_list("cen_sb", cen)
 
         x_plane = keep.tile([P, S], U8, name="x_plane", align_bytes=64)
         nc.gpsimd.memset(x_plane[:].bitcast(I32), 0)
-
         picked_scales = keep.tile([P, S], U8, name="picked_scales", align_bytes=64)
         nc.vector.tensor_copy(picked_scales[:], scale_table[:].indirect(offs_sb[:]))
+
+        w1_view = w1_raw[:].rearrange("p j (m t) -> p m t j", t=PACK)
+        dealt = keep.tile([P, PACK, P, PACK], BF16, name="dealt", tag="dealt", align_bytes=64)
+        dealt_view = dealt[:].rearrange("p t m j -> p m t j")
         for q in range(QUADS):
             nc.scalar.dma_start(
                 x_plane[32 * q : 32 * q + 4, :].bitcast(I32),
                 picked_scales[32 + 16 * q : 48 + 16 * q : 4, :].bitcast(I32),
             )
-
-        x_codes = []
-        for part in range(S // BANK):
-            codes = keep.tile([P, BANK], U32, name="x_codes%d" % part, align_bytes=64)
-            nc.vector.tensor_copy(codes[:], x_table[:].indirect(entries(offs_sb, part * BANK, (part + 1) * BANK)))
-            x_codes.append(codes)
-
-        for n in range(2):
-            spare = psum_out.tile([P, BANK], F32, name="spare", tag="out_acc%d" % n)
-            nc.tensor.matmul_mx(
-                spare[:], lhsT=x_codes[0][:, 0:P].bitcast(FP8X4), lhsT_scale=picked_scales[:, 0:P],
-                rhs=x_codes[0][:].bitcast(FP8X4), rhs_scale=picked_scales[:, 0:BANK], start=True, stop=True,
-            )
-
-        w1_view = w1_raw[:].rearrange("p j (m t) -> p m t j", t=PACK)
-        dealt_outer = keep.tile([P, 2, P, PACK], BF16, name="dealt_outer", tag="dealt_outer", align_bytes=64)
-        dealt_inner = keep.tile([P, 2, P, PACK], BF16, name="dealt_inner", align_bytes=64)
-        outer_view = dealt_outer[:].rearrange("p t m j -> p m t j")
+        for g in range(2):
+            nc.vector.tensor_copy(dealt_view[:, :, 2 * g : 2 * g + 2, :], w1_view[:, :, 2 * g : 2 * g + 2, :])
         w1_codes = keep.tile([P, PACK * P], U32, name="w1_codes", align_bytes=64)
         w1_plane = keep.tile([P, PACK * P], U8, name="w1_plane", align_bytes=64)
-
-        def quantize_w1(first_tile, end_tile, dealt):
-            cols = slice(first_tile * P, end_tile * P)
+        for g in range(2):
+            cols = slice(2 * g * P, (2 * g + 2) * P)
             nc.vector.quantize_mx(
-                w1_codes[:, cols].bitcast(FP8X4), w1_plane[:, cols], dealt.rearrange("p t m j -> p (t m j)")
+                w1_codes[:, cols].bitcast(FP8X4), w1_plane[:, cols],
+                dealt[:, 2 * g : 2 * g + 2].rearrange("p t m j -> p (t m j)"),
             )
 
-        nc.scalar.activation(outer_view[:, :, :, 0:2], w1_view[:, :, 0:PACK:3, 0:2], COPY)
-        for place, t in enumerate((0, 3)):
-            nc.scalar.activation(outer_view[:, :, place, 2:4], w1_view[:, :, t, 2:4], COPY)
-        nc.vector.tensor_copy(dealt_inner[:].rearrange("p t m j -> p m t j"), w1_view[:, :, 1:3, :])
-        quantize_w1(0, 1, dealt_outer[:, 0:1])
-        quantize_w1(1, 3, dealt_inner[:])
+        x_codes = keep.tile([P, S], U32, name="x_codes", align_bytes=64)
+        for lo in range(0, S, PIECE):
+            nc.vector.tensor_copy(x_codes[:, lo : lo + PIECE], x_table[:].indirect(entries(offs_sb, lo, lo + PIECE)))
 
         h = [keep.tile([P, S], F32, name="h%d" % t) for t in range(PACK)]
-        for t in range(PACK):
-            lo = 0
-            for piece, width in enumerate(FIRST_PIECES if t == 0 else LATER_PIECES):
-                acc = psum_h.tile([P, width], F32, name="acc")
-                nc.tensor.matmul_mx(
-                    acc[:],
-                    lhsT=w1_codes[:, t * P : (t + 1) * P].bitcast(FP8X4),
-                    lhsT_scale=w1_plane[:, t * P : (t + 1) * P],
-                    rhs=x_codes[lo // BANK][:, lo % BANK : lo % BANK + width].bitcast(FP8X4),
-                    rhs_scale=x_plane[:, lo : lo + width],
-                    start=True,
-                    stop=True,
-                )
-                if t == 0 and piece in VECTOR_PIECES:
-                    nc.vector.tensor_scalar_max(h[t][:, lo : lo + width], acc[:], 0.0)
-                else:
-                    nc.scalar.activation(h[t][:, lo : lo + width], acc[:], RELU)
-                lo = lo + width
-            if t == 0:
-                quantize_w1(3, 4, dealt_outer[:, 1:2])
+
+        def first_product(t, lo, hi, on_vector):
+            acc = psum_h.tile([P, hi - lo], F32, name="acc")
+            nc.tensor.matmul_mx(
+                acc[:],
+                lhsT=w1_codes[:, t * P : (t + 1) * P].bitcast(FP8X4),
+                lhsT_scale=w1_plane[:, t * P : (t + 1) * P],
+                rhs=x_codes[:, lo:hi].bitcast(FP8X4),
+                rhs_scale=x_plane[:, lo:hi],
+                start=True,
+                stop=True,
+            )
+            if on_vector:
+                nc.vector.tensor_scalar_max(h[t][:, lo:hi], acc[:], 0.0)
+            else:
+                nc.scalar.activation(h[t][:, lo:hi], acc[:], RELU)
+
+        for lo in range(0, S - PIECE, PIECE):
+            for t in range(2):
+                first_product(t, lo, lo + PIECE, False)
+        first_product(0, S - PIECE, S - PIECE // 2, True)
+        first_product(0, S - PIECE // 2, S, False)
+        first_product(1, S - PIECE, S, False)
+        for t in range(2, PACK):
+            for lo in range(0, S, 2 * PIECE):
+                first_product(t, lo, lo + 2 * PIECE, False)
 
         tail_codes = keep.tile([P, 2, N], U32, name="tail_codes", tag="w1_raw", align_bytes=64)
-        tail_planes = keep.tile([P, 2, N], U8, name="tail_planes", tag="dealt_outer", align_bytes=64)
+        tail_planes = keep.tile([P, 2, N], U8, name="tail_planes", tag="dealt", align_bytes=64)
         nc.gpsimd.memset(tail_planes[:].rearrange("p w n -> p (w n)").bitcast(I32), 0)
-        for w, (words, scales) in enumerate(((w3_words, w3_scales), (w2_words, w2_scales))):
+        for w, (words, scales) in enumerate(((w2_words, w2_scales), (w3_words, w3_scales))):
             nc.sync.dma_start(tail_codes[:, w, :].bitcast(I32), words[0].rearrange("p n j -> p (n j)").bitcast(I32))
             for q in range(QUADS):
                 nc.sync.dma_start(
                     tail_planes[32 * q : 32 * q + 4, w, :].bitcast(I32), scales[0, 4 * q : 4 * q + 4, :].bitcast(I32)
                 )
 
-        def interleave(grouped, source):
-            nc.scalar.copy(
+        def on_vector(dst, t, lst, lo, hi):
+            nc.vector.tensor_copy(dst, h[t][:].indirect(entries(lst, lo, hi)))
+
+        def on_scalar(dst, t, lst, lo, hi):
+            nc.scalar.activation(dst, h[t][:].indirect(entries(lst, lo, hi)), COPY)
+
+        def pool_interleave(grouped, source):
+            nc.gpsimd.tensor_scalar(grouped, source.rearrange("p t v -> p v t"), 1.0, 0.0, MULT, ADD)
+
+        def vector_interleave(grouped, source):
+            nc.vector.tensor_copy(
                 grouped.rearrange("p (c i) t -> p c t i", i=4), source.rearrange("p t (c i) -> p c t i", i=4)
             )
 
@@ -159,86 +150,81 @@ def tile_picked_sagecat_max_p_kernel(
             nc.vector.quantize_mx(codes[:].bitcast(FP8X4), plane[:], grouped.rearrange("p v t -> p (v t)"))
             return codes, plane
 
-        def fetch(dst, t, lst, lo, hi):
-            nc.vector.tensor_copy(dst, h[t][:].indirect(entries(lst, lo, hi)))
+        def pair_tile(name, tag):
+            return keep.tile([P, 2, HALF], BF16, name=name, tag=tag)
 
-        def larger(dst, a, b, t):
-            diff = keep.tile([P, V], F32, name="diff%d" % t, tag="diff", bufs=2)
-            nc.gpsimd.tensor_tensor(diff[:], b, a, SUB)
-            gain = keep.tile([P, V], F32, name="gain%d" % t)
-            nc.scalar.activation(gain[:], diff[:], RELU)
-            nc.gpsimd.tensor_tensor(dst, a, gain[:], ADD)
-
-        z = keep.tile([P, PACK, V], BF16, name="z")
-        rows = keep.tile([P, 2 * PACK, V], BF16, name="rows")
-        rows_b = rows[:, 0:PACK, :]
-        rows_a = rows[:, PACK : 2 * PACK, :]
-
-        for t in range(PACK):
-            fetch(rows_a[:, t, :], t, pos_sb[0], 0, V)
-            fetch(rows_b[:, t, :], t, pos_sb[1], 0, V)
-            if t < PACK // 2:
-                larger(z[:, t, :], rows_a[:, t, :], rows_b[:, t, :], t)
-            else:
-                larger(z[:, t, :], rows_b[:, t, :], rows_a[:, t, :], t)
-        for t in range(PACK):
-            fetch(rows_a[:, t, :], t, pos_sb[2], 0, V)
-        own_grouped = keep.tile([P, V, PACK], BF16, name="own_grouped", align_bytes=64)
         out_acc = [
             psum_out.tile([P, hi - lo], F32, name="out_acc%d" % c, tag="out_acc%d" % c)
             for c, (lo, hi) in enumerate(CHUNKS)
         ]
 
-        def fetch_own(c, dst, tiles):
-            lo, hi = CHUNKS[c]
-            for t in tiles:
-                fetch(dst[:, t, :], t, cen_sb, lo, hi)
-
-        def quantize_z(u):
-            codes, plane = quantize("z%d" % u, z_grouped[u][:], HALF)
-            for c, (lo, hi) in enumerate(CHUNKS):
-                if lo // HALF == u:
-                    cols = slice(lo % HALF, lo % HALF + hi - lo)
-                    nc.tensor.matmul_mx(
-                        out_acc[c][:], lhsT=tail_codes[:, 0, :].bitcast(FP8X4), lhsT_scale=tail_planes[:, 0, :],
-                        rhs=codes[:, cols].bitcast(FP8X4), rhs_scale=plane[:, cols], start=True, stop=False,
-                    )
-
-        own_first = rows[:, 2:6, 0:HALF]
-        fetch_own(0, own_first, range(1))
-        nc.vector.tensor_tensor(z[:], z[:], rows_a, MAX)
-        z_grouped = []
-        for u in range(2):
-            grouped = keep.tile([P, HALF, PACK], BF16, name="z_grouped%d" % u, tag="z_grouped%d" % u, align_bytes=64)
-            interleave(grouped[:], z[:, :, u * HALF : (u + 1) * HALF])
-            z_grouped.append(grouped)
-        fetch_own(0, own_first, range(1, PACK))
-        nc.gpsimd.tensor_scalar(own_grouped[:, 0:HALF, :], own_first.rearrange("p t v -> p v t"), 1.0, 0.0, MULT, ADD)
-        quantize_z(0)
-
-        lo, hi = CHUNKS[1]
-        own_second = z[:, :, lo - HALF : hi - HALF]
-        fetch_own(1, own_second, range(PACK))
-        interleave(own_grouped[:, lo:hi, :], own_second)
-        lo, hi = CHUNKS[2]
-        own_third = z[:, :, lo - HALF : hi - HALF]
-        fetch_own(2, own_third, range(PACK - 1))
-        for at in range(0, hi - lo, LAST_PIECE):
-            piece_cols = slice(at, at + LAST_PIECE)
-            fetch(own_third[:, PACK - 1, piece_cols], PACK - 1, cen_sb, lo + at, lo + at + LAST_PIECE)
-            interleave(own_grouped[:, lo + at : lo + at + LAST_PIECE, :], own_third[:, :, piece_cols])
-
-        for c, (lo, hi) in enumerate(CHUNKS):
-            if lo == HALF:
-                quantize_z(1)
-            own_codes, own_plane = quantize("own%d" % c, own_grouped[:, lo:hi, :], hi - lo)
+        def second_product(c, w, codes, plane):
             nc.tensor.matmul_mx(
-                out_acc[c][:], lhsT=tail_codes[:, 1, :].bitcast(FP8X4), lhsT_scale=tail_planes[:, 1, :],
-                rhs=own_codes[:].bitcast(FP8X4), rhs_scale=own_plane[:], start=False, stop=True,
+                out_acc[c][:], lhsT=tail_codes[:, w, :].bitcast(FP8X4), lhsT_scale=tail_planes[:, w, :],
+                rhs=codes.bitcast(FP8X4), rhs_scale=plane, start=w == 0, stop=w == 1,
             )
+
+        def store(c, engine_copy):
+            lo, hi = CHUNKS[c]
             result = keep.tile([P, hi - lo], F32, name="result%d" % c)
-            if hi == V:
-                nc.vector.tensor_copy(result[:], out_acc[c][:])
-            else:
-                nc.scalar.copy(result[:], out_acc[c][:])
+            engine_copy(result[:], out_acc[c][:])
             nc.sync.dma_start(out[:, lo:hi], result[:])
+
+        own = keep.tile([P, PACK, V], BF16, name="own")
+        for t in range(PACK):
+            (on_vector if t < 2 else on_scalar)(own[:, t, :], t, cen_sb, 0, V)
+        own_grouped = keep.tile([P, V, PACK], BF16, name="own_grouped", align_bytes=64)
+        for lo in range(0, V, HALF):
+            pool_interleave(own_grouped[:, lo : lo + HALF, :], own[:, :, lo : lo + HALF])
+
+        first = [[pair_tile("first%d%d" % (d, g), "first%d%d" % (d, g)) for g in range(2)] for d in range(3)]
+        for t in range(PACK):
+            for d in range(3):
+                (on_vector if t < 3 else on_scalar)(first[d][t // 2][:, t % 2, :], t, pos_sb[d], 0, HALF)
+        larger = [pair_tile("larger%d" % g, "larger%d" % g) for g in range(2)]
+        z_first = keep.tile([P, PACK, HALF], BF16, name="z_first")
+        for g in range(2):
+            nc.vector.tensor_tensor(larger[g][:], first[0][g][:], first[1][g][:], MAX)
+        for g in range(2):
+            nc.vector.tensor_tensor(z_first[:, 2 * g : 2 * g + 2, :], larger[g][:], first[2][g][:], MAX)
+        z_first_grouped = keep.tile([P, HALF, PACK], BF16, name="z_first_grouped", align_bytes=64)
+        pool_interleave(z_first_grouped[:], z_first[:])
+
+        low = [pair_tile("low0", "first21"), pair_tile("low1", "larger1"), pair_tile("low2", "first20")]
+        high = [pair_tile("high%d" % d, "high%d" % d) for d in range(3)]
+        for d in range(3):
+            on_vector(low[d][:, 0, :], 0, pos_sb[d], HALF, V)
+        for d in range(2):
+            for t in range(2, PACK):
+                on_scalar(high[d][:, t % 2, :], t, pos_sb[d], HALF, V)
+        on_scalar(high[2][:, 0, :], 2, pos_sb[2], HALF, V)
+        for d in range(2):
+            on_scalar(low[d][:, 1, :], 1, pos_sb[d], HALF, V)
+        on_scalar(high[2][:, 1, :], 3, pos_sb[2], HALF, V)
+        for lo in range(0, HALF, QUARTER):
+            on_scalar(low[2][:, 1, lo : lo + QUARTER], 1, pos_sb[2], HALF + lo, HALF + lo + QUARTER)
+
+        own_codes, own_plane = quantize("own", own_grouped[:], V)
+        for c, (lo, hi) in enumerate(CHUNKS):
+            second_product(c, 0, own_codes[:, lo:hi], own_plane[:, lo:hi])
+        codes, plane = quantize("z0", z_first_grouped[:], HALF)
+        second_product(0, 1, codes[:], plane[:])
+
+        z_second = keep.tile([P, PACK, HALF], BF16, name="z_second")
+        larger_high = pair_tile("larger_high", "larger_high")
+        larger_low = pair_tile("larger_low", "larger_low")
+        nc.vector.tensor_tensor(larger_high[:], high[0][:], high[1][:], MAX)
+        nc.vector.tensor_tensor(larger_low[:], low[0][:], low[1][:], MAX)
+        nc.vector.tensor_tensor(z_second[:, 2:4, :], larger_high[:], high[2][:], MAX)
+        store(0, nc.scalar.copy)
+        grouped = []
+        for u in range(2):
+            cols = slice(u * QUARTER, (u + 1) * QUARTER)
+            nc.vector.tensor_tensor(z_second[:, 0:2, cols], larger_low[:, :, cols], low[2][:, :, cols], MAX)
+            tile = keep.tile([P, QUARTER, PACK], BF16, name="z_grouped%d" % u, align_bytes=64)
+            vector_interleave(tile[:], z_second[:, :, cols])
+            grouped.append(tile)
+        for u in range(2):
+            codes, plane = quantize("z%d" % (u + 1), grouped[u][:], QUARTER)
+            second_product(u + 1, 1, codes[:], plane[:])
+            store(u + 1, nc.vector.tensor_copy if u == 1 else nc.scalar.copy)

@@ -23,7 +23,11 @@ P = 128
 PACK = 4
 QUADS = 4
 LIST_ROWS = 16
-PIECE = 256
+BANK = 512
+X_HEAD = 1536
+FIRST_PIECES = (256, 256, 256, 128, 128)
+VECTOR_PIECES = (0, 2)
+LATER_PIECES = (256, 256, 256, 256)
 H_BANKS = 5
 HALF = V // 2
 QUARTER = V // 4
@@ -50,78 +54,92 @@ def tile_picked_sagecat_max_p_kernel(
         scale_table = keep.tile([P, T], U8, name="scale_table")
         nc.gpsimd.memset(scale_table[:, 0 : T // 2].bitcast(I32), 0)
         nc.vector.memset(scale_table[:, T // 2 : T].bitcast(I32), 0)
+        idle = keep.tile([P, 16], F32, name="idle")
+        nc.gpsimd.memset(idle[:, 0:8], 0.0)
+        nc.scalar.activation(idle[:, 8:9], idle[:, 0:1], RELU)
 
+        x_rows = x_words[0].rearrange("p n j -> p (n j)").bitcast(I32)
+        x_table = keep.tile([P, T], U32, name="x_table")
+        nc.sync.dma_start(x_table[:, 0:X_HEAD].bitcast(I32), x_rows[:, 0:X_HEAD])
+        offs_sb = load_list("offs_sb", offs)
+        pos_sb = [load_list("pos0_sb", pos1), load_list("pos1_sb", pos2)]
+        nc.sync.dma_start(scale_table[32:96:4, :].bitcast(I32), x_scales[0].bitcast(I32))
+        nc.sync.dma_start(x_table[:, X_HEAD:T].bitcast(I32), x_rows[:, X_HEAD:T])
         w1_rows = w1.rearrange("(p j) c -> p j c", j=PACK)
         w1_raw = keep.tile([P, PACK, H], F32, name="w1_raw", tag="w1_raw", align_bytes=64)
-        nc.sync.dma_start(w1_raw[:, 0:2, :], w1_rows[:, 0:2, :])
-        offs_sb = load_list("offs_sb", offs)
-        pos_sb = [load_list("pos0_sb", pos1)]
-        nc.sync.dma_start(scale_table[32:96:4, :].bitcast(I32), x_scales[0].bitcast(I32))
-        nc.sync.dma_start(w1_raw[:, 2:4, :], w1_rows[:, 2:4, :])
-        x_table = keep.tile([P, T], U32, name="x_table")
-        nc.sync.dma_start(x_table[:].bitcast(I32), x_words[0].rearrange("p n j -> p (n j)").bitcast(I32))
-        pos_sb.append(load_list("pos1_sb", pos2))
+        for pair in range(2):
+            nc.sync.dma_start(w1_raw[:, 2 * pair : 2 * pair + 2, :], w1_rows[:, 2 * pair : 2 * pair + 2, :])
         pos_sb.append(load_list("pos2_sb", pos3))
         cen_sb = load_list("cen_sb", cen)
 
         x_plane = keep.tile([P, S], U8, name="x_plane", align_bytes=64)
         nc.gpsimd.memset(x_plane[:].bitcast(I32), 0)
+
         picked_scales = keep.tile([P, S], U8, name="picked_scales", align_bytes=64)
         nc.vector.tensor_copy(picked_scales[:], scale_table[:].indirect(offs_sb[:]))
-
-        w1_view = w1_raw[:].rearrange("p j (m t) -> p m t j", t=PACK)
-        dealt = keep.tile([P, PACK, P, PACK], BF16, name="dealt", tag="dealt", align_bytes=64)
-        dealt_view = dealt[:].rearrange("p t m j -> p m t j")
         for q in range(QUADS):
             nc.scalar.dma_start(
                 x_plane[32 * q : 32 * q + 4, :].bitcast(I32),
                 picked_scales[32 + 16 * q : 48 + 16 * q : 4, :].bitcast(I32),
             )
-        for g in range(2):
-            nc.vector.tensor_copy(dealt_view[:, :, 2 * g : 2 * g + 2, :], w1_view[:, :, 2 * g : 2 * g + 2, :])
+
+        x_codes = []
+        for part in range(S // BANK):
+            codes = keep.tile([P, BANK], U32, name="x_codes%d" % part, align_bytes=64)
+            nc.vector.tensor_copy(codes[:], x_table[:].indirect(entries(offs_sb, part * BANK, (part + 1) * BANK)))
+            x_codes.append(codes)
+
+        for n in range(1):
+            spare = psum_out.tile([P, BANK], F32, name="spare", tag="out_acc%d" % n)
+            nc.tensor.matmul_mx(
+                spare[:], lhsT=x_codes[0][:, 0:P].bitcast(FP8X4), lhsT_scale=picked_scales[:, 0:P],
+                rhs=x_codes[0][:].bitcast(FP8X4), rhs_scale=picked_scales[:, 0:BANK], start=True, stop=True,
+            )
+
+        w1_view = w1_raw[:].rearrange("p j (m t) -> p m t j", t=PACK)
+        dealt_outer = keep.tile([P, 2, P, PACK], BF16, name="dealt_outer", tag="dealt_outer", align_bytes=64)
+        dealt_inner = keep.tile([P, 2, P, PACK], BF16, name="dealt_inner", align_bytes=64)
+        outer_view = dealt_outer[:].rearrange("p t m j -> p m t j")
         w1_codes = keep.tile([P, PACK * P], U32, name="w1_codes", align_bytes=64)
         w1_plane = keep.tile([P, PACK * P], U8, name="w1_plane", align_bytes=64)
-        for g in range(2):
-            cols = slice(2 * g * P, (2 * g + 2) * P)
+
+        def quantize_w1(first_tile, end_tile, dealt):
+            cols = slice(first_tile * P, end_tile * P)
             nc.vector.quantize_mx(
-                w1_codes[:, cols].bitcast(FP8X4), w1_plane[:, cols],
-                dealt[:, 2 * g : 2 * g + 2].rearrange("p t m j -> p (t m j)"),
+                w1_codes[:, cols].bitcast(FP8X4), w1_plane[:, cols], dealt.rearrange("p t m j -> p (t m j)")
             )
 
-        x_codes = keep.tile([P, S], U32, name="x_codes", align_bytes=64)
-        for lo in range(0, S, PIECE):
-            nc.vector.tensor_copy(x_codes[:, lo : lo + PIECE], x_table[:].indirect(entries(offs_sb, lo, lo + PIECE)))
+        nc.scalar.activation(outer_view[:, :, :, 0:2], w1_view[:, :, 0:PACK:3, 0:2], COPY)
+        for place, t in enumerate((0, 3)):
+            nc.scalar.activation(outer_view[:, :, place, 2:4], w1_view[:, :, t, 2:4], COPY)
+        nc.vector.tensor_copy(dealt_inner[:].rearrange("p t m j -> p m t j"), w1_view[:, :, 1:3, :])
+        quantize_w1(0, 1, dealt_outer[:, 0:1])
+        quantize_w1(1, 3, dealt_inner[:])
 
         h = [keep.tile([P, S], F32, name="h%d" % t) for t in range(PACK)]
-
-        def first_product(t, lo, hi, on_vector):
-            acc = psum_h.tile([P, hi - lo], F32, name="acc")
-            nc.tensor.matmul_mx(
-                acc[:],
-                lhsT=w1_codes[:, t * P : (t + 1) * P].bitcast(FP8X4),
-                lhsT_scale=w1_plane[:, t * P : (t + 1) * P],
-                rhs=x_codes[:, lo:hi].bitcast(FP8X4),
-                rhs_scale=x_plane[:, lo:hi],
-                start=True,
-                stop=True,
-            )
-            if on_vector:
-                nc.vector.tensor_scalar_max(h[t][:, lo:hi], acc[:], 0.0)
-            else:
-                nc.scalar.activation(h[t][:, lo:hi], acc[:], RELU)
-
-        for lo in range(0, S - PIECE, PIECE):
-            for t in range(2):
-                first_product(t, lo, lo + PIECE, False)
-        first_product(0, S - PIECE, S - PIECE // 2, True)
-        first_product(0, S - PIECE // 2, S, False)
-        first_product(1, S - PIECE, S, False)
-        for t in range(2, PACK):
-            for lo in range(0, S, 2 * PIECE):
-                first_product(t, lo, lo + 2 * PIECE, False)
+        for t in range(PACK):
+            lo = 0
+            for piece, width in enumerate(FIRST_PIECES if t == 0 else LATER_PIECES):
+                acc = psum_h.tile([P, width], F32, name="acc")
+                nc.tensor.matmul_mx(
+                    acc[:],
+                    lhsT=w1_codes[:, t * P : (t + 1) * P].bitcast(FP8X4),
+                    lhsT_scale=w1_plane[:, t * P : (t + 1) * P],
+                    rhs=x_codes[lo // BANK][:, lo % BANK : lo % BANK + width].bitcast(FP8X4),
+                    rhs_scale=x_plane[:, lo : lo + width],
+                    start=True,
+                    stop=True,
+                )
+                if t == 0 and piece in VECTOR_PIECES:
+                    nc.vector.tensor_scalar_max(h[t][:, lo : lo + width], acc[:], 0.0)
+                else:
+                    nc.scalar.activation(h[t][:, lo : lo + width], acc[:], RELU)
+                lo = lo + width
+            if t == 0:
+                quantize_w1(3, 4, dealt_outer[:, 1:2])
 
         tail_codes = keep.tile([P, 2, N], U32, name="tail_codes", tag="w1_raw", align_bytes=64)
-        tail_planes = keep.tile([P, 2, N], U8, name="tail_planes", tag="dealt", align_bytes=64)
+        tail_planes = keep.tile([P, 2, N], U8, name="tail_planes", tag="dealt_outer", align_bytes=64)
         nc.gpsimd.memset(tail_planes[:].rearrange("p w n -> p (w n)").bitcast(I32), 0)
         for w, (words, scales) in enumerate(((w2_words, w2_scales), (w3_words, w3_scales))):
             nc.sync.dma_start(tail_codes[:, w, :].bitcast(I32), words[0].rearrange("p n j -> p (n j)").bitcast(I32))
@@ -135,9 +153,6 @@ def tile_picked_sagecat_max_p_kernel(
 
         def on_scalar(dst, t, lst, lo, hi):
             nc.scalar.activation(dst, h[t][:].indirect(entries(lst, lo, hi)), COPY)
-
-        def pool_interleave(grouped, source):
-            nc.gpsimd.tensor_scalar(grouped, source.rearrange("p t v -> p v t"), 1.0, 0.0, MULT, ADD)
 
         def vector_interleave(grouped, source):
             nc.vector.tensor_copy(
@@ -174,13 +189,12 @@ def tile_picked_sagecat_max_p_kernel(
         for t in range(PACK):
             (on_vector if t < 2 else on_scalar)(own[:, t, :], t, cen_sb, 0, V)
         own_grouped = keep.tile([P, V, PACK], BF16, name="own_grouped", align_bytes=64)
-        for lo in range(0, V, HALF):
-            pool_interleave(own_grouped[:, lo : lo + HALF, :], own[:, :, lo : lo + HALF])
 
         first = [[pair_tile("first%d%d" % (d, g), "first%d%d" % (d, g)) for g in range(2)] for d in range(3)]
         for t in range(PACK):
             for d in range(3):
                 (on_vector if t < 3 else on_scalar)(first[d][t // 2][:, t % 2, :], t, pos_sb[d], 0, HALF)
+        vector_interleave(own_grouped[:], own[:])
         larger = [pair_tile("larger%d" % g, "larger%d" % g) for g in range(2)]
         z_first = keep.tile([P, PACK, HALF], BF16, name="z_first")
         for g in range(2):
@@ -188,25 +202,26 @@ def tile_picked_sagecat_max_p_kernel(
         for g in range(2):
             nc.vector.tensor_tensor(z_first[:, 2 * g : 2 * g + 2, :], larger[g][:], first[2][g][:], MAX)
         z_first_grouped = keep.tile([P, HALF, PACK], BF16, name="z_first_grouped", align_bytes=64)
-        pool_interleave(z_first_grouped[:], z_first[:])
+        own_codes, own_plane = quantize("own", own_grouped[:], V)
+        for c, (lo, hi) in enumerate(CHUNKS):
+            second_product(c, 0, own_codes[:, lo:hi], own_plane[:, lo:hi])
+        vector_interleave(z_first_grouped[:], z_first[:])
 
-        low = [pair_tile("low0", "first21"), pair_tile("low1", "larger1"), pair_tile("low2", "first20")]
+        low = [pair_tile("low0", "first21"), pair_tile("low1", "low1"), pair_tile("low2", "low2")]
         high = [pair_tile("high%d" % d, "high%d" % d) for d in range(3)]
-        for d in range(3):
-            on_vector(low[d][:, 0, :], 0, pos_sb[d], HALF, V)
         for d in range(2):
             for t in range(2, PACK):
                 on_scalar(high[d][:, t % 2, :], t, pos_sb[d], HALF, V)
+        for t in range(2):
+            on_scalar(low[1][:, t, :], t, pos_sb[1], HALF, V)
+        on_vector(low[0][:, 0, :], 0, pos_sb[0], HALF, V)
+        on_scalar(low[0][:, 1, :], 1, pos_sb[0], HALF, V)
         on_scalar(high[2][:, 0, :], 2, pos_sb[2], HALF, V)
-        for d in range(2):
-            on_scalar(low[d][:, 1, :], 1, pos_sb[d], HALF, V)
+        on_scalar(low[2][:, 0, :], 0, pos_sb[2], HALF, V)
         on_scalar(high[2][:, 1, :], 3, pos_sb[2], HALF, V)
         for lo in range(0, HALF, QUARTER):
             on_scalar(low[2][:, 1, lo : lo + QUARTER], 1, pos_sb[2], HALF + lo, HALF + lo + QUARTER)
 
-        own_codes, own_plane = quantize("own", own_grouped[:], V)
-        for c, (lo, hi) in enumerate(CHUNKS):
-            second_product(c, 0, own_codes[:, lo:hi], own_plane[:, lo:hi])
         codes, plane = quantize("z0", z_first_grouped[:], HALF)
         second_product(0, 1, codes[:], plane[:])
 

@@ -154,13 +154,14 @@ def tile_picked_sagecat_max_p_kernel(
         def on_scalar(dst, t, lst, lo, hi):
             nc.scalar.activation(dst, h[t][:].indirect(entries(lst, lo, hi)), COPY)
 
-        def vector_interleave(grouped, source):
-            nc.vector.tensor_copy(
-                grouped.rearrange("p (c i) t -> p c t i", i=4), source.rearrange("p t (c i) -> p c t i", i=4)
-            )
+        def grouped_view(grouped):
+            return grouped.rearrange("p (c i) t -> p c t i", i=4)
 
-        def quantize(name, grouped, width):
-            codes = keep.tile([P, width], U32, name=name + "_codes", align_bytes=64)
+        def rows_view(source):
+            return source.rearrange("p t (c i) -> p c t i", i=4)
+
+        def quantize(name, grouped, width, tag):
+            codes = keep.tile([P, width], U32, name=name + "_codes", tag=tag, align_bytes=64)
             plane = keep.tile([P, width], U8, name=name + "_plane", align_bytes=64)
             nc.vector.quantize_mx(codes[:].bitcast(FP8X4), plane[:], grouped.rearrange("p v t -> p (v t)"))
             return codes, plane
@@ -173,10 +174,10 @@ def tile_picked_sagecat_max_p_kernel(
             for c, (lo, hi) in enumerate(CHUNKS)
         ]
 
-        def second_product(c, w, codes, plane):
+        def second_product(c, w, codes, plane, opens):
             nc.tensor.matmul_mx(
                 out_acc[c][:], lhsT=tail_codes[:, w, :].bitcast(FP8X4), lhsT_scale=tail_planes[:, w, :],
-                rhs=codes.bitcast(FP8X4), rhs_scale=plane, start=w == 0, stop=w == 1,
+                rhs=codes.bitcast(FP8X4), rhs_scale=plane, start=opens, stop=not opens,
             )
 
         def store(c, engine_copy):
@@ -185,61 +186,65 @@ def tile_picked_sagecat_max_p_kernel(
             engine_copy(result[:], out_acc[c][:])
             nc.sync.dma_start(out[:, lo:hi], result[:])
 
-        own = keep.tile([P, PACK, V], BF16, name="own")
-        for t in range(PACK):
-            (on_vector if t < 2 else on_scalar)(own[:, t, :], t, cen_sb, 0, V)
-        own_grouped = keep.tile([P, V, PACK], BF16, name="own_grouped", align_bytes=64)
+        EARLY = HALF + QUARTER
+        own = [keep.tile([P, 2, EARLY], BF16, name="own%d" % g, tag="own%d" % g) for g in range(2)]
+        own_grouped = keep.tile([P, EARLY, PACK], BF16, name="own_grouped", align_bytes=64)
+        for g, fetch in enumerate((on_vector, on_scalar)):
+            for t in range(2):
+                fetch(own[g][:, t, :], 2 * g + t, cen_sb, 0, EARLY)
+            nc.gpsimd.tensor_scalar(
+                own_grouped[:, :, 2 * g : 2 * g + 2], own[g][:].rearrange("p t v -> p v t"), 1.0, 0.0, MULT, ADD
+            )
 
         first = [[pair_tile("first%d%d" % (d, g), "first%d%d" % (d, g)) for g in range(2)] for d in range(3)]
         for t in range(PACK):
             for d in range(3):
                 (on_vector if t < 3 else on_scalar)(first[d][t // 2][:, t % 2, :], t, pos_sb[d], 0, HALF)
-        vector_interleave(own_grouped[:], own[:])
-        larger = [pair_tile("larger%d" % g, "larger%d" % g) for g in range(2)]
-        z_first = keep.tile([P, PACK, HALF], BF16, name="z_first")
-        for g in range(2):
-            nc.vector.tensor_tensor(larger[g][:], first[0][g][:], first[1][g][:], MAX)
-        for g in range(2):
-            nc.vector.tensor_tensor(z_first[:, 2 * g : 2 * g + 2, :], larger[g][:], first[2][g][:], MAX)
-        z_first_grouped = keep.tile([P, HALF, PACK], BF16, name="z_first_grouped", align_bytes=64)
-        own_codes, own_plane = quantize("own", own_grouped[:], V)
-        for c, (lo, hi) in enumerate(CHUNKS):
-            second_product(c, 0, own_codes[:, lo:hi], own_plane[:, lo:hi])
-        vector_interleave(z_first_grouped[:], z_first[:])
 
-        low = [pair_tile("low0", "first21"), pair_tile("low1", "low1"), pair_tile("low2", "low2")]
+        larger_first = keep.tile([P, 2, 2, HALF], BF16, name="larger_first", tag="own1")
+        z_first = keep.tile([P, PACK, HALF], BF16, name="z_first", tag="z_first")
+        for g in range(2):
+            nc.vector.tensor_tensor(larger_first[:, g], first[0][g][:], first[1][g][:], MAX)
+        own_codes, own_plane = quantize("own", own_grouped[:], EARLY, "own_codes")
+        for c in range(2):
+            lo, hi = CHUNKS[c]
+            second_product(c, 0, own_codes[:, lo:hi], own_plane[:, lo:hi], True)
+        for g in range(2):
+            nc.vector.tensor_tensor(z_first[:, 2 * g : 2 * g + 2, :], larger_first[:, g], first[2][g][:], MAX)
+        grouped_first = keep.tile([P, HALF, PACK], BF16, name="grouped_first", align_bytes=64)
+        nc.gpsimd.tensor_scalar(grouped_first[:], z_first[:].rearrange("p t v -> p v t"), 1.0, 0.0, MULT, ADD)
+
+        low = [pair_tile("low0", "first20"), pair_tile("low1", "first21"), pair_tile("low2", "low2")]
         high = [pair_tile("high%d" % d, "high%d" % d) for d in range(3)]
         for d in range(2):
+            for t in range(2):
+                on_vector(low[d][:, t, :], t, pos_sb[d], HALF, V)
+        for d in range(3):
             for t in range(2, PACK):
                 on_scalar(high[d][:, t % 2, :], t, pos_sb[d], HALF, V)
         for t in range(2):
-            on_scalar(low[1][:, t, :], t, pos_sb[1], HALF, V)
-        on_vector(low[0][:, 0, :], 0, pos_sb[0], HALF, V)
-        on_scalar(low[0][:, 1, :], 1, pos_sb[0], HALF, V)
-        on_scalar(high[2][:, 0, :], 2, pos_sb[2], HALF, V)
-        on_scalar(low[2][:, 0, :], 0, pos_sb[2], HALF, V)
-        on_scalar(high[2][:, 1, :], 3, pos_sb[2], HALF, V)
-        for lo in range(0, HALF, QUARTER):
-            on_scalar(low[2][:, 1, lo : lo + QUARTER], 1, pos_sb[2], HALF + lo, HALF + lo + QUARTER)
+            on_scalar(low[2][:, t, :], t, pos_sb[2], HALF, V)
+        own_last = keep.tile([P, PACK, QUARTER], BF16, name="own_last")
+        for t in range(PACK):
+            on_scalar(own_last[:, t, :], t, cen_sb, EARLY, V)
+        last_grouped = keep.tile([P, QUARTER, PACK], BF16, name="last_grouped", align_bytes=64)
+        nc.scalar.copy(grouped_view(last_grouped[:]), rows_view(own_last[:]))
 
-        codes, plane = quantize("z0", z_first_grouped[:], HALF)
-        second_product(0, 1, codes[:], plane[:])
-
-        z_second = keep.tile([P, PACK, HALF], BF16, name="z_second")
-        larger_high = pair_tile("larger_high", "larger_high")
-        larger_low = pair_tile("larger_low", "larger_low")
-        nc.vector.tensor_tensor(larger_high[:], high[0][:], high[1][:], MAX)
-        nc.vector.tensor_tensor(larger_low[:], low[0][:], low[1][:], MAX)
-        nc.vector.tensor_tensor(z_second[:, 2:4, :], larger_high[:], high[2][:], MAX)
+        codes, plane = quantize("z0", grouped_first[:], HALF, "z0_codes")
+        second_product(0, 1, codes[:], plane[:], False)
+        larger_second = keep.tile([P, 2, 2, HALF], BF16, name="larger_second", tag="z_first")
+        z_second = keep.tile([P, PACK, HALF], BF16, name="z_second", tag="z_second", align_bytes=64)
+        for g, rows in ((1, high), (0, low)):
+            nc.vector.tensor_tensor(larger_second[:, g], rows[0][:], rows[1][:], MAX)
+        for g, rows in ((1, high), (0, low)):
+            nc.vector.tensor_tensor(z_second[:, 2 * g : 2 * g + 2, :], larger_second[:, g], rows[2][:], MAX)
+        grouped_second = keep.tile([P, HALF, PACK], BF16, name="grouped_second", align_bytes=64)
+        nc.vector.tensor_copy(grouped_view(grouped_second[:]), rows_view(z_second[:]))
         store(0, nc.scalar.copy)
-        grouped = []
-        for u in range(2):
-            cols = slice(u * QUARTER, (u + 1) * QUARTER)
-            nc.vector.tensor_tensor(z_second[:, 0:2, cols], larger_low[:, :, cols], low[2][:, :, cols], MAX)
-            tile = keep.tile([P, QUARTER, PACK], BF16, name="z_grouped%d" % u, align_bytes=64)
-            vector_interleave(tile[:], z_second[:, :, cols])
-            grouped.append(tile)
-        for u in range(2):
-            codes, plane = quantize("z%d" % (u + 1), grouped[u][:], QUARTER)
-            second_product(u + 1, 1, codes[:], plane[:])
-            store(u + 1, nc.vector.tensor_copy if u == 1 else nc.scalar.copy)
+        codes, plane = quantize("z1", grouped_second[:], HALF, "z1_codes")
+        second_product(1, 1, codes[:, 0:QUARTER], plane[:, 0:QUARTER], False)
+        second_product(2, 1, codes[:, QUARTER:HALF], plane[:, QUARTER:HALF], True)
+        store(1, nc.scalar.copy)
+        codes, plane = quantize("last", last_grouped[:], QUARTER, "z_second")
+        second_product(2, 0, codes[:], plane[:], False)
+        store(2, nc.vector.tensor_copy)

@@ -26,8 +26,8 @@ LIST_ROWS = 16
 BANK = 512
 X_HEAD = 1536
 FIRST_PIECES = (256, 256, 256, 128, 128)
-VECTOR_PIECES = (0, 2)
-LATER_PIECES = (256, 256, 256, 256)
+VECTOR_PIECES = (3,)
+LATER_PIECES = (512, 512)
 H_BANKS = 5
 HALF = V // 2
 QUARTER = V // 4
@@ -97,9 +97,8 @@ def tile_picked_sagecat_max_p_kernel(
             )
 
         w1_view = w1_raw[:].rearrange("p j (m t) -> p m t j", t=PACK)
-        dealt_outer = keep.tile([P, 2, P, PACK], BF16, name="dealt_outer", tag="dealt_outer", align_bytes=64)
-        dealt_inner = keep.tile([P, 2, P, PACK], BF16, name="dealt_inner", align_bytes=64)
-        outer_view = dealt_outer[:].rearrange("p t m j -> p m t j")
+        dealt = keep.tile([P, 3, P, PACK], BF16, name="dealt", tag="dealt_outer", align_bytes=64)
+        outer_view = dealt[:, 0:3:2].rearrange("p t m j -> p m t j")
         w1_codes = keep.tile([P, PACK * P], U32, name="w1_codes", align_bytes=64)
         w1_plane = keep.tile([P, PACK * P], U8, name="w1_plane", align_bytes=64)
 
@@ -112,14 +111,15 @@ def tile_picked_sagecat_max_p_kernel(
         nc.scalar.activation(outer_view[:, :, :, 0:2], w1_view[:, :, 0:PACK:3, 0:2], COPY)
         for place, t in enumerate((0, 3)):
             nc.scalar.activation(outer_view[:, :, place, 2:4], w1_view[:, :, t, 2:4], COPY)
-        nc.vector.tensor_copy(dealt_inner[:].rearrange("p t m j -> p m t j"), w1_view[:, :, 1:3, :])
-        quantize_w1(0, 1, dealt_outer[:, 0:1])
-        quantize_w1(1, 3, dealt_inner[:])
+        quantize_w1(0, 1, dealt[:, 0:1])
+        nc.vector.tensor_copy(dealt[:, 0:2].rearrange("p t m j -> p m t j"), w1_view[:, :, 1:3, :])
+        quantize_w1(3, 4, dealt[:, 2:3])
+        quantize_w1(1, 3, dealt[:, 0:2])
 
         h = [keep.tile([P, S], F32, name="h%d" % t) for t in range(PACK)]
         for t in range(PACK):
             lo = 0
-            for piece, width in enumerate(FIRST_PIECES if t == 0 else LATER_PIECES):
+            for piece, width in enumerate(FIRST_PIECES if t == 0 else (256, 256, 512) if t == 1 else LATER_PIECES):
                 acc = psum_h.tile([P, width], F32, name="acc")
                 nc.tensor.matmul_mx(
                     acc[:],
@@ -135,8 +135,6 @@ def tile_picked_sagecat_max_p_kernel(
                 else:
                     nc.scalar.activation(h[t][:, lo : lo + width], acc[:], RELU)
                 lo = lo + width
-            if t == 0:
-                quantize_w1(3, 4, dealt_outer[:, 1:2])
 
         tail_codes = keep.tile([P, 2, N], U32, name="tail_codes", tag="w1_raw", align_bytes=64)
         tail_planes = keep.tile([P, 2, N], U8, name="tail_planes", tag="dealt_outer", align_bytes=64)
@@ -187,13 +185,13 @@ def tile_picked_sagecat_max_p_kernel(
             nc.sync.dma_start(out[:, lo:hi], result[:])
 
         EARLY = HALF + QUARTER
-        own = [keep.tile([P, 2, EARLY], BF16, name="own%d" % g, tag="own%d" % g) for g in range(2)]
-        own_grouped = keep.tile([P, EARLY, PACK], BF16, name="own_grouped", align_bytes=64)
-        for g, fetch in enumerate((on_vector, on_scalar)):
+        own_grouped = keep.tile([P, V, PACK], BF16, name="own_grouped", align_bytes=64)
+        for g, (fetch, width) in enumerate(((on_vector, V), (on_scalar, EARLY))):
+            own = keep.tile([P, 2, width], BF16, name="own%d" % g, tag="own%d" % g)
             for t in range(2):
-                fetch(own[g][:, t, :], 2 * g + t, cen_sb, 0, EARLY)
+                fetch(own[:, t, :], 2 * g + t, cen_sb, 0, width)
             nc.gpsimd.tensor_scalar(
-                own_grouped[:, :, 2 * g : 2 * g + 2], own[g][:].rearrange("p t v -> p v t"), 1.0, 0.0, MULT, ADD
+                own_grouped[:, 0:width, 2 * g : 2 * g + 2], own[:].rearrange("p t v -> p v t"), 1.0, 0.0, MULT, ADD
             )
 
         first = [[pair_tile("first%d%d" % (d, g), "first%d%d" % (d, g)) for g in range(2)] for d in range(3)]
@@ -202,20 +200,20 @@ def tile_picked_sagecat_max_p_kernel(
                 (on_vector if t < 3 else on_scalar)(first[d][t // 2][:, t % 2, :], t, pos_sb[d], 0, HALF)
 
         larger_first = keep.tile([P, 2, 2, HALF], BF16, name="larger_first", tag="own1")
-        z_first = keep.tile([P, PACK, HALF], BF16, name="z_first", tag="z_first")
+        z_first = keep.tile([P, PACK, HALF], BF16, name="z_first", tag="z_first", align_bytes=64)
         for g in range(2):
             nc.vector.tensor_tensor(larger_first[:, g], first[0][g][:], first[1][g][:], MAX)
-        own_codes, own_plane = quantize("own", own_grouped[:], EARLY, "own_codes")
+        own_codes, own_plane = quantize("own", own_grouped[:, 0:EARLY, :], EARLY, "own_codes")
         for c in range(2):
             lo, hi = CHUNKS[c]
             second_product(c, 0, own_codes[:, lo:hi], own_plane[:, lo:hi], True)
         for g in range(2):
-            nc.vector.tensor_tensor(z_first[:, 2 * g : 2 * g + 2, :], larger_first[:, g], first[2][g][:], MAX)
+            nc.vector.tensor_tensor(z_first[:, 2 * g : 2 * g + 2, :], larger_first[:, g], first[2][g][:, :, :], MAX)
         grouped_first = keep.tile([P, HALF, PACK], BF16, name="grouped_first", align_bytes=64)
         nc.gpsimd.tensor_scalar(grouped_first[:], z_first[:].rearrange("p t v -> p v t"), 1.0, 0.0, MULT, ADD)
 
-        low = [pair_tile("low0", "first20"), pair_tile("low1", "first21"), pair_tile("low2", "low2")]
-        high = [pair_tile("high%d" % d, "high%d" % d) for d in range(3)]
+        low = [pair_tile("low0", "first21")[:], pair_tile("low1", "first20")[:], pair_tile("low2", "low2")[:]]
+        high = [pair_tile("high%d" % d, "high%d" % d)[:] for d in range(3)]
         for d in range(2):
             for t in range(2):
                 on_vector(low[d][:, t, :], t, pos_sb[d], HALF, V)
@@ -224,27 +222,32 @@ def tile_picked_sagecat_max_p_kernel(
                 on_scalar(high[d][:, t % 2, :], t, pos_sb[d], HALF, V)
         for t in range(2):
             on_scalar(low[2][:, t, :], t, pos_sb[2], HALF, V)
-        own_last = keep.tile([P, PACK, QUARTER], BF16, name="own_last")
-        for t in range(PACK):
-            on_scalar(own_last[:, t, :], t, cen_sb, EARLY, V)
-        last_grouped = keep.tile([P, QUARTER, PACK], BF16, name="last_grouped", align_bytes=64)
-        nc.scalar.copy(grouped_view(last_grouped[:]), rows_view(own_last[:]))
+        own_last = keep.tile([P, 2, QUARTER], BF16, name="own_last")
+        for t in range(2):
+            on_scalar(own_last[:, t, :], 2 + t, cen_sb, EARLY, V)
+        nc.scalar.copy(grouped_view(own_grouped[:, EARLY:V, 2:4]), rows_view(own_last[:]))
 
         codes, plane = quantize("z0", grouped_first[:], HALF, "z0_codes")
         second_product(0, 1, codes[:], plane[:], False)
-        larger_second = keep.tile([P, 2, 2, HALF], BF16, name="larger_second", tag="z_first")
+        larger_second = keep.tile([P, 2, 2, HALF], BF16, name="larger_second", tag="z_first", align_bytes=64)
         z_second = keep.tile([P, PACK, HALF], BF16, name="z_second", tag="z_second", align_bytes=64)
         for g, rows in ((1, high), (0, low)):
-            nc.vector.tensor_tensor(larger_second[:, g], rows[0][:], rows[1][:], MAX)
-        for g, rows in ((1, high), (0, low)):
-            nc.vector.tensor_tensor(z_second[:, 2 * g : 2 * g + 2, :], larger_second[:, g], rows[2][:], MAX)
-        grouped_second = keep.tile([P, HALF, PACK], BF16, name="grouped_second", align_bytes=64)
-        nc.vector.tensor_copy(grouped_view(grouped_second[:]), rows_view(z_second[:]))
+            nc.vector.tensor_tensor(larger_second[:, g], rows[0], rows[1], MAX)
+        nc.vector.tensor_tensor(z_second[:, 2:4, :], larger_second[:, 1], high[2], MAX)
+        quarters = [slice(u * QUARTER, (u + 1) * QUARTER) for u in range(2)]
+        for cols in quarters:
+            nc.vector.tensor_tensor(z_second[:, 0:2, cols], larger_second[:, 0, :, cols], low[2][:, :, cols], MAX)
         store(0, nc.scalar.copy)
-        codes, plane = quantize("z1", grouped_second[:], HALF, "z1_codes")
-        second_product(1, 1, codes[:, 0:QUARTER], plane[:, 0:QUARTER], False)
-        second_product(2, 1, codes[:, QUARTER:HALF], plane[:, QUARTER:HALF], True)
+        grouped_second = []
+        for u, cols in enumerate(quarters):
+            grouped = keep.tile([P, QUARTER, PACK], BF16, name="grouped_second%d" % u, align_bytes=64)
+            nc.vector.tensor_copy(grouped_view(grouped[:]), rows_view(z_second[:, :, cols]))
+            grouped_second.append(grouped)
+        codes, plane = quantize("z1", grouped_second[0][:], QUARTER, "z1_codes")
+        second_product(1, 1, codes[:], plane[:], False)
         store(1, nc.scalar.copy)
-        codes, plane = quantize("last", last_grouped[:], QUARTER, "z_second")
-        second_product(2, 0, codes[:], plane[:], False)
+        codes, plane = quantize("last", own_grouped[:, EARLY:V, :], QUARTER, "z_second")
+        second_product(2, 0, codes[:], plane[:], True)
+        codes, plane = quantize("z2", grouped_second[1][:], QUARTER, "z2_codes")
+        second_product(2, 1, codes[:], plane[:], False)
         store(2, nc.vector.tensor_copy)

@@ -13,7 +13,6 @@ U16 = mybir.dt.uint16
 U8 = mybir.dt.uint8
 FP8X4 = mybir.dt.float8_e4m3fn_x4
 MAX = mybir.AluOpType.max
-SUB = mybir.AluOpType.subtract
 ADD = mybir.AluOpType.add
 MULT = mybir.AluOpType.mult
 COPY = mybir.ActivationFunctionType.Copy
@@ -23,15 +22,17 @@ P = 128
 PACK = 4
 QUADS = 4
 LIST_ROWS = 16
+NEIGHBOURS = 3
 BANK = 512
 X_HEAD = 1536
-FIRST_PIECES = (256, 256, 256, 128, 128)
-VECTOR_PIECES = (3,)
-LATER_PIECES = (512, 512)
+PIECES = ((256, 256, 256, 128, 128), (256, 256, 512), (512, 512), (512, 512))
+VECTOR_PIECE = 3
 H_BANKS = 5
 HALF = V // 2
 QUARTER = V // 4
-CHUNKS = ((0, HALF), (HALF, HALF + QUARTER), (HALF + QUARTER, V))
+EARLY = HALF + QUARTER
+CHUNKS = ((0, HALF), (HALF, EARLY), (EARLY, V))
+W2, W3 = 0, 1
 
 
 def tile_picked_sagecat_max_p_kernel(
@@ -89,23 +90,16 @@ def tile_picked_sagecat_max_p_kernel(
             nc.vector.tensor_copy(codes[:], x_table[:].indirect(entries(offs_sb, part * BANK, (part + 1) * BANK)))
             x_codes.append(codes)
 
-        for n in range(1):
-            spare = psum_out.tile([P, BANK], F32, name="spare", tag="out_acc%d" % n)
-            nc.tensor.matmul_mx(
-                spare[:], lhsT=x_codes[0][:, 0:P].bitcast(FP8X4), lhsT_scale=picked_scales[:, 0:P],
-                rhs=x_codes[0][:].bitcast(FP8X4), rhs_scale=picked_scales[:, 0:BANK], start=True, stop=True,
-            )
-
         w1_view = w1_raw[:].rearrange("p j (m t) -> p m t j", t=PACK)
-        dealt = keep.tile([P, 3, P, PACK], BF16, name="dealt", tag="dealt_outer", align_bytes=64)
+        dealt = keep.tile([P, 3, P, PACK], BF16, name="dealt", tag="dealt", align_bytes=64)
         outer_view = dealt[:, 0:3:2].rearrange("p t m j -> p m t j")
         w1_codes = keep.tile([P, PACK * P], U32, name="w1_codes", align_bytes=64)
         w1_plane = keep.tile([P, PACK * P], U8, name="w1_plane", align_bytes=64)
 
-        def quantize_w1(first_tile, end_tile, dealt):
+        def quantize_w1(first_tile, end_tile, source):
             cols = slice(first_tile * P, end_tile * P)
             nc.vector.quantize_mx(
-                w1_codes[:, cols].bitcast(FP8X4), w1_plane[:, cols], dealt.rearrange("p t m j -> p (t m j)")
+                w1_codes[:, cols].bitcast(FP8X4), w1_plane[:, cols], source.rearrange("p t m j -> p (t m j)")
             )
 
         nc.scalar.activation(outer_view[:, :, :, 0:2], w1_view[:, :, 0:PACK:3, 0:2], COPY)
@@ -119,7 +113,7 @@ def tile_picked_sagecat_max_p_kernel(
         h = [keep.tile([P, S], F32, name="h%d" % t) for t in range(PACK)]
         for t in range(PACK):
             lo = 0
-            for piece, width in enumerate(FIRST_PIECES if t == 0 else (256, 256, 512) if t == 1 else LATER_PIECES):
+            for piece, width in enumerate(PIECES[t]):
                 acc = psum_h.tile([P, width], F32, name="acc")
                 nc.tensor.matmul_mx(
                     acc[:],
@@ -130,33 +124,33 @@ def tile_picked_sagecat_max_p_kernel(
                     start=True,
                     stop=True,
                 )
-                if t == 0 and piece in VECTOR_PIECES:
+                if (t, piece) == (0, VECTOR_PIECE):
                     nc.vector.tensor_scalar_max(h[t][:, lo : lo + width], acc[:], 0.0)
                 else:
                     nc.scalar.activation(h[t][:, lo : lo + width], acc[:], RELU)
                 lo = lo + width
 
         tail_codes = keep.tile([P, 2, N], U32, name="tail_codes", tag="w1_raw", align_bytes=64)
-        tail_planes = keep.tile([P, 2, N], U8, name="tail_planes", tag="dealt_outer", align_bytes=64)
+        tail_planes = keep.tile([P, 2, N], U8, name="tail_planes", tag="dealt", align_bytes=64)
         nc.gpsimd.memset(tail_planes[:].rearrange("p w n -> p (w n)").bitcast(I32), 0)
-        for w, (words, scales) in enumerate(((w2_words, w2_scales), (w3_words, w3_scales))):
+        for w, words, scales in ((W2, w2_words, w2_scales), (W3, w3_words, w3_scales)):
             nc.sync.dma_start(tail_codes[:, w, :].bitcast(I32), words[0].rearrange("p n j -> p (n j)").bitcast(I32))
             for q in range(QUADS):
                 nc.sync.dma_start(
                     tail_planes[32 * q : 32 * q + 4, w, :].bitcast(I32), scales[0, 4 * q : 4 * q + 4, :].bitcast(I32)
                 )
 
-        def on_vector(dst, t, lst, lo, hi):
+        def fetch_on_vector(dst, t, lst, lo, hi):
             nc.vector.tensor_copy(dst, h[t][:].indirect(entries(lst, lo, hi)))
 
-        def on_scalar(dst, t, lst, lo, hi):
+        def fetch_on_scalar(dst, t, lst, lo, hi):
             nc.scalar.activation(dst, h[t][:].indirect(entries(lst, lo, hi)), COPY)
 
-        def grouped_view(grouped):
-            return grouped.rearrange("p (c i) t -> p c t i", i=4)
+        def group_on_gpsimd(grouped, rows):
+            nc.gpsimd.tensor_scalar(grouped, rows.rearrange("p t v -> p v t"), 1.0, 0.0, MULT, ADD)
 
-        def rows_view(source):
-            return source.rearrange("p t (c i) -> p c t i", i=4)
+        def group_with(engine_copy, grouped, rows):
+            engine_copy(grouped.rearrange("p (c i) t -> p c t i", i=4), rows.rearrange("p t (c i) -> p c t i", i=4))
 
         def quantize(name, grouped, width, tag):
             codes = keep.tile([P, width], U32, name=name + "_codes", tag=tag, align_bytes=64)
@@ -172,10 +166,10 @@ def tile_picked_sagecat_max_p_kernel(
             for c, (lo, hi) in enumerate(CHUNKS)
         ]
 
-        def second_product(c, w, codes, plane, opens):
+        def second_product(c, w, codes, plane):
             nc.tensor.matmul_mx(
                 out_acc[c][:], lhsT=tail_codes[:, w, :].bitcast(FP8X4), lhsT_scale=tail_planes[:, w, :],
-                rhs=codes.bitcast(FP8X4), rhs_scale=plane, start=opens, stop=not opens,
+                rhs=codes.bitcast(FP8X4), rhs_scale=plane, start=w == W2, stop=w == W3,
             )
 
         def store(c, engine_copy):
@@ -184,20 +178,18 @@ def tile_picked_sagecat_max_p_kernel(
             engine_copy(result[:], out_acc[c][:])
             nc.sync.dma_start(out[:, lo:hi], result[:])
 
-        EARLY = HALF + QUARTER
         own_grouped = keep.tile([P, V, PACK], BF16, name="own_grouped", align_bytes=64)
-        for g, (fetch, width) in enumerate(((on_vector, V), (on_scalar, EARLY))):
+        for g, (fetch, width) in enumerate(((fetch_on_vector, V), (fetch_on_scalar, EARLY))):
             own = keep.tile([P, 2, width], BF16, name="own%d" % g, tag="own%d" % g)
             for t in range(2):
                 fetch(own[:, t, :], 2 * g + t, cen_sb, 0, width)
-            nc.gpsimd.tensor_scalar(
-                own_grouped[:, 0:width, 2 * g : 2 * g + 2], own[:].rearrange("p t v -> p v t"), 1.0, 0.0, MULT, ADD
-            )
+            group_on_gpsimd(own_grouped[:, 0:width, 2 * g : 2 * g + 2], own[:])
 
-        first = [[pair_tile("first%d%d" % (d, g), "first%d%d" % (d, g)) for g in range(2)] for d in range(3)]
+        first = [[pair_tile("first%d%d" % (d, g), "first%d%d" % (d, g)) for g in range(2)] for d in range(NEIGHBOURS)]
         for t in range(PACK):
-            for d in range(3):
-                (on_vector if t < 3 else on_scalar)(first[d][t // 2][:, t % 2, :], t, pos_sb[d], 0, HALF)
+            fetch = fetch_on_vector if t < PACK - 1 else fetch_on_scalar
+            for d in range(NEIGHBOURS):
+                fetch(first[d][t // 2][:, t % 2, :], t, pos_sb[d], 0, HALF)
 
         larger_first = keep.tile([P, 2, 2, HALF], BF16, name="larger_first", tag="own1")
         z_first = keep.tile([P, PACK, HALF], BF16, name="z_first", tag="z_first", align_bytes=64)
@@ -206,48 +198,48 @@ def tile_picked_sagecat_max_p_kernel(
         own_codes, own_plane = quantize("own", own_grouped[:, 0:EARLY, :], EARLY, "own_codes")
         for c in range(2):
             lo, hi = CHUNKS[c]
-            second_product(c, 0, own_codes[:, lo:hi], own_plane[:, lo:hi], True)
+            second_product(c, W2, own_codes[:, lo:hi], own_plane[:, lo:hi])
         for g in range(2):
-            nc.vector.tensor_tensor(z_first[:, 2 * g : 2 * g + 2, :], larger_first[:, g], first[2][g][:, :, :], MAX)
-        grouped_first = keep.tile([P, HALF, PACK], BF16, name="grouped_first", align_bytes=64)
-        nc.gpsimd.tensor_scalar(grouped_first[:], z_first[:].rearrange("p t v -> p v t"), 1.0, 0.0, MULT, ADD)
+            nc.vector.tensor_tensor(z_first[:, 2 * g : 2 * g + 2, :], larger_first[:, g], first[2][g][:], MAX)
+        z_first_grouped = keep.tile([P, HALF, PACK], BF16, name="z_first_grouped", align_bytes=64)
+        group_on_gpsimd(z_first_grouped[:], z_first[:])
 
-        low = [pair_tile("low0", "first21")[:], pair_tile("low1", "first20")[:], pair_tile("low2", "low2")[:]]
-        high = [pair_tile("high%d" % d, "high%d" % d)[:] for d in range(3)]
+        low = [pair_tile("low0", "first21"), pair_tile("low1", "first20"), pair_tile("low2", "low2")]
+        high = [pair_tile("high%d" % d, "high%d" % d) for d in range(NEIGHBOURS)]
         for d in range(2):
             for t in range(2):
-                on_vector(low[d][:, t, :], t, pos_sb[d], HALF, V)
-        for d in range(3):
-            for t in range(2, PACK):
-                on_scalar(high[d][:, t % 2, :], t, pos_sb[d], HALF, V)
+                fetch_on_vector(low[d][:, t, :], t, pos_sb[d], HALF, V)
+        for d in range(NEIGHBOURS):
+            for t in range(2):
+                fetch_on_scalar(high[d][:, t, :], 2 + t, pos_sb[d], HALF, V)
         for t in range(2):
-            on_scalar(low[2][:, t, :], t, pos_sb[2], HALF, V)
+            fetch_on_scalar(low[2][:, t, :], t, pos_sb[2], HALF, V)
         own_last = keep.tile([P, 2, QUARTER], BF16, name="own_last")
         for t in range(2):
-            on_scalar(own_last[:, t, :], 2 + t, cen_sb, EARLY, V)
-        nc.scalar.copy(grouped_view(own_grouped[:, EARLY:V, 2:4]), rows_view(own_last[:]))
+            fetch_on_scalar(own_last[:, t, :], 2 + t, cen_sb, EARLY, V)
+        group_with(nc.scalar.copy, own_grouped[:, EARLY:V, 2:4], own_last[:])
 
-        codes, plane = quantize("z0", grouped_first[:], HALF, "z0_codes")
-        second_product(0, 1, codes[:], plane[:], False)
+        codes, plane = quantize("z0", z_first_grouped[:], HALF, "z0_codes")
+        second_product(0, W3, codes[:], plane[:])
         larger_second = keep.tile([P, 2, 2, HALF], BF16, name="larger_second", tag="z_first", align_bytes=64)
         z_second = keep.tile([P, PACK, HALF], BF16, name="z_second", tag="z_second", align_bytes=64)
         for g, rows in ((1, high), (0, low)):
-            nc.vector.tensor_tensor(larger_second[:, g], rows[0], rows[1], MAX)
-        nc.vector.tensor_tensor(z_second[:, 2:4, :], larger_second[:, 1], high[2], MAX)
+            nc.vector.tensor_tensor(larger_second[:, g], rows[0][:], rows[1][:], MAX)
+        nc.vector.tensor_tensor(z_second[:, 2:4, :], larger_second[:, 1], high[2][:], MAX)
         quarters = [slice(u * QUARTER, (u + 1) * QUARTER) for u in range(2)]
         for cols in quarters:
             nc.vector.tensor_tensor(z_second[:, 0:2, cols], larger_second[:, 0, :, cols], low[2][:, :, cols], MAX)
         store(0, nc.scalar.copy)
-        grouped_second = []
+        z_second_grouped = []
         for u, cols in enumerate(quarters):
-            grouped = keep.tile([P, QUARTER, PACK], BF16, name="grouped_second%d" % u, align_bytes=64)
-            nc.vector.tensor_copy(grouped_view(grouped[:]), rows_view(z_second[:, :, cols]))
-            grouped_second.append(grouped)
-        codes, plane = quantize("z1", grouped_second[0][:], QUARTER, "z1_codes")
-        second_product(1, 1, codes[:], plane[:], False)
+            grouped = keep.tile([P, QUARTER, PACK], BF16, name="z_second_grouped%d" % u, align_bytes=64)
+            group_with(nc.vector.tensor_copy, grouped[:], z_second[:, :, cols])
+            z_second_grouped.append(grouped)
+        codes, plane = quantize("z1", z_second_grouped[0][:], QUARTER, "z1_codes")
+        second_product(1, W3, codes[:], plane[:])
         store(1, nc.scalar.copy)
         codes, plane = quantize("last", own_grouped[:, EARLY:V, :], QUARTER, "z_second")
-        second_product(2, 0, codes[:], plane[:], True)
-        codes, plane = quantize("z2", grouped_second[1][:], QUARTER, "z2_codes")
-        second_product(2, 1, codes[:], plane[:], False)
+        second_product(2, W2, codes[:], plane[:])
+        codes, plane = quantize("z2", z_second_grouped[1][:], QUARTER, "z2_codes")
+        second_product(2, W3, codes[:], plane[:])
         store(2, nc.vector.tensor_copy)

@@ -26,7 +26,7 @@ NEIGHBOURS = 3
 BANK = 512
 X_HEAD = 1536
 PIECES = ((256, 256, 256, 128, 128), (256, 256, 512), (512, 512), (512, 512))
-VECTOR_PIECE = 3
+VECTOR_PIECES = (0, 3)
 H_BANKS = 5
 HALF = V // 2
 QUARTER = V // 4
@@ -91,24 +91,33 @@ def tile_picked_sagecat_max_p_kernel(
             x_codes.append(codes)
 
         w1_view = w1_raw[:].rearrange("p j (m t) -> p m t j", t=PACK)
-        dealt = keep.tile([P, 3, P, PACK], BF16, name="dealt", tag="dealt", align_bytes=64)
-        outer_view = dealt[:, 0:3:2].rearrange("p t m j -> p m t j")
+        dealt = keep.tile([P, PACK, P, PACK], BF16, name="dealt", tag="dealt", align_bytes=64)
+        dealt_view = dealt[:].rearrange("p t m j -> p m t j")
         w1_codes = keep.tile([P, PACK * P], U32, name="w1_codes", align_bytes=64)
         w1_plane = keep.tile([P, PACK * P], U8, name="w1_plane", align_bytes=64)
 
-        def quantize_w1(first_tile, end_tile, source):
+        def quantize_w1(first_tile, end_tile):
             cols = slice(first_tile * P, end_tile * P)
-            nc.vector.quantize_mx(
-                w1_codes[:, cols].bitcast(FP8X4), w1_plane[:, cols], source.rearrange("p t m j -> p (t m j)")
+            source = dealt[:, first_tile:end_tile].rearrange("p t m j -> p (t m j)")
+            nc.vector.quantize_mx(w1_codes[:, cols].bitcast(FP8X4), w1_plane[:, cols], source)
+
+        def round_on_scalar(places, tiles, pair):
+            nc.scalar.activation(dealt_view[:, places, tiles, pair], w1_view[:, places, tiles, pair], COPY)
+
+        def round_on_gpsimd(places, tiles, pair):
+            nc.gpsimd.tensor_scalar(
+                dealt_view[:, places, tiles, pair], w1_view[:, places, tiles, pair], 1.0, 0.0, MULT, ADD
             )
 
-        nc.scalar.activation(outer_view[:, :, :, 0:2], w1_view[:, :, 0:PACK:3, 0:2], COPY)
-        for place, t in enumerate((0, 3)):
-            nc.scalar.activation(outer_view[:, :, place, 2:4], w1_view[:, :, t, 2:4], COPY)
-        quantize_w1(0, 1, dealt[:, 0:1])
-        nc.vector.tensor_copy(dealt[:, 0:2].rearrange("p t m j -> p m t j"), w1_view[:, :, 1:3, :])
-        quantize_w1(3, 4, dealt[:, 2:3])
-        quantize_w1(1, 3, dealt[:, 0:2])
+        early, late = slice(0, 2), slice(2, 4)
+        every, low, high = slice(0, P), slice(0, P // 2), slice(P // 2, P)
+        round_on_scalar(every, slice(0, 2), early)
+        round_on_gpsimd(every, slice(2, 4), early)
+        round_on_scalar(low, 0, late)
+        round_on_gpsimd(high, 0, late)
+        round_on_scalar(every, slice(1, 4), late)
+        quantize_w1(0, 1)
+        quantize_w1(1, 4)
 
         h = [keep.tile([P, S], F32, name="h%d" % t) for t in range(PACK)]
         for t in range(PACK):
@@ -124,7 +133,7 @@ def tile_picked_sagecat_max_p_kernel(
                     start=True,
                     stop=True,
                 )
-                if (t, piece) == (0, VECTOR_PIECE):
+                if t == 0 and piece in VECTOR_PIECES:
                     nc.vector.tensor_scalar_max(h[t][:, lo : lo + width], acc[:], 0.0)
                 else:
                     nc.scalar.activation(h[t][:, lo : lo + width], acc[:], RELU)

@@ -63,15 +63,14 @@ def tile_picked_sagecat_max_p_kernel(
         x_table = keep.tile([P, T], U32, name="x_table")
         nc.sync.dma_start(x_table[:, 0:X_HEAD].bitcast(I32), x_rows[:, 0:X_HEAD])
         offs_sb = load_list("offs_sb", offs)
-        pos_sb = [load_list("pos0_sb", pos1), load_list("pos1_sb", pos2)]
         nc.sync.dma_start(scale_table[32:96:4, :].bitcast(I32), x_scales[0].bitcast(I32))
         nc.sync.dma_start(x_table[:, X_HEAD:T].bitcast(I32), x_rows[:, X_HEAD:T])
         w1_rows = w1.rearrange("(p j) c -> p j c", j=PACK)
         w1_raw = keep.tile([P, PACK, H], F32, name="w1_raw", tag="w1_raw", align_bytes=64)
         for pair in range(2):
             nc.sync.dma_start(w1_raw[:, 2 * pair : 2 * pair + 2, :], w1_rows[:, 2 * pair : 2 * pair + 2, :])
-        pos_sb.append(load_list("pos2_sb", pos3))
         cen_sb = load_list("cen_sb", cen)
+        pos_sb = [load_list("pos0_sb", pos1)]
 
         x_plane = keep.tile([P, S], U8, name="x_plane", align_bytes=64)
         nc.gpsimd.memset(x_plane[:].bitcast(I32), 0)
@@ -84,11 +83,9 @@ def tile_picked_sagecat_max_p_kernel(
                 picked_scales[32 + 16 * q : 48 + 16 * q : 4, :].bitcast(I32),
             )
 
-        x_codes = []
-        for part in range(S // BANK):
-            codes = keep.tile([P, BANK], U32, name="x_codes%d" % part, align_bytes=64)
-            nc.vector.tensor_copy(codes[:], x_table[:].indirect(entries(offs_sb, part * BANK, (part + 1) * BANK)))
-            x_codes.append(codes)
+        pos_sb.extend([load_list("pos1_sb", pos2), load_list("pos2_sb", pos3)])
+        x_codes = keep.tile([P, S], U32, name="x_codes", align_bytes=64)
+        nc.vector.tensor_copy(x_codes[:], x_table[:].indirect(offs_sb[:]))
 
         w1_view = w1_raw[:].rearrange("p j (m t) -> p m t j", t=PACK)
         dealt = keep.tile([P, PACK, P, PACK], BF16, name="dealt", tag="dealt", align_bytes=64)
@@ -128,7 +125,7 @@ def tile_picked_sagecat_max_p_kernel(
                     acc[:],
                     lhsT=w1_codes[:, t * P : (t + 1) * P].bitcast(FP8X4),
                     lhsT_scale=w1_plane[:, t * P : (t + 1) * P],
-                    rhs=x_codes[lo // BANK][:, lo % BANK : lo % BANK + width].bitcast(FP8X4),
+                    rhs=x_codes[:, lo : lo + width].bitcast(FP8X4),
                     rhs_scale=x_plane[:, lo : lo + width],
                     start=True,
                     stop=True,

@@ -26,7 +26,7 @@ NEIGHBOURS = 3
 BANK = 512
 X_HEAD = 1536
 PIECES = ((256, 256, 256, 128, 128), (256, 256, 512), (512, 512), (512, 512))
-VECTOR_PIECES = (0, 3)
+VECTOR_PIECES = (0, 1, 3)
 H_BANKS = 5
 HALF = V // 2
 QUARTER = V // 4
@@ -112,9 +112,10 @@ def tile_picked_sagecat_max_p_kernel(
         round_on_gpsimd(every, slice(2, 4), early)
         round_on_scalar(low, 0, late)
         round_on_gpsimd(high, 0, late)
-        round_on_scalar(every, slice(1, 4), late)
+        round_on_scalar(every, 1, late)
+        round_on_scalar(every, slice(2, 4), late)
         quantize_w1(0, 1)
-        quantize_w1(1, 4)
+        quantize_w1(1, 2)
 
         h = [keep.tile([P, S], F32, name="h%d" % t) for t in range(PACK)]
         for t in range(PACK):
@@ -135,6 +136,8 @@ def tile_picked_sagecat_max_p_kernel(
                 else:
                     nc.scalar.activation(h[t][:, lo : lo + width], acc[:], RELU)
                 lo = lo + width
+                if t == 0 and piece == 3:
+                    quantize_w1(2, 4)
 
         tail_codes = keep.tile([P, 2, N], U32, name="tail_codes", tag="w1_raw", align_bytes=64)
         tail_planes = keep.tile([P, 2, N], U8, name="tail_planes", tag="dealt", align_bytes=64)
@@ -164,9 +167,6 @@ def tile_picked_sagecat_max_p_kernel(
             nc.vector.quantize_mx(codes[:].bitcast(FP8X4), plane[:], grouped.rearrange("p v t -> p (v t)"))
             return codes, plane
 
-        def pair_tile(name, tag):
-            return keep.tile([P, 2, HALF], BF16, name=name, tag=tag)
-
         out_acc = [
             psum_out.tile([P, hi - lo], F32, name="out_acc%d" % c, tag="out_acc%d" % c)
             for c, (lo, hi) in enumerate(CHUNKS)
@@ -178,74 +178,74 @@ def tile_picked_sagecat_max_p_kernel(
                 rhs=codes.bitcast(FP8X4), rhs_scale=plane, start=w == W2, stop=w == W3,
             )
 
-        def store(c, engine_copy):
+        def store(c, engine_copy, tag):
             lo, hi = CHUNKS[c]
-            result = keep.tile([P, hi - lo], F32, name="result%d" % c)
+            result = keep.tile([P, hi - lo], F32, name="result%d" % c, tag=tag)
             engine_copy(result[:], out_acc[c][:])
             nc.sync.dma_start(out[:, lo:hi], result[:])
 
-        own_grouped = keep.tile([P, V, PACK], BF16, name="own_grouped", align_bytes=64)
-        for g, (fetch, width) in enumerate(((fetch_on_vector, V), (fetch_on_scalar, EARLY))):
-            own = keep.tile([P, 2, width], BF16, name="own%d" % g, tag="own%d" % g)
-            for t in range(2):
-                fetch(own[:, t, :], 2 * g + t, cen_sb, 0, width)
-            group_on_gpsimd(own_grouped[:, 0:width, 2 * g : 2 * g + 2], own[:])
+        own_early = keep.tile([P, EARLY, PACK], BF16, name="own_early", tag="own_early", align_bytes=64)
+        own_late = keep.tile([P, QUARTER, PACK], BF16, name="own_late", align_bytes=64)
+        own_low = keep.tile([P, 2, V], BF16, name="own_low")
+        own_high = keep.tile([P, 2, EARLY], BF16, name="own_high", tag="own_high")
+        for t in range(2):
+            fetch_on_vector(own_low[:, t, :], t, cen_sb, 0, V)
+            fetch_on_scalar(own_high[:, t, :], 2 + t, cen_sb, 0, EARLY)
+        group_on_gpsimd(own_early[:, :, 0:2], own_low[:, :, 0:EARLY])
+        group_on_gpsimd(own_late[:, :, 0:2], own_low[:, :, EARLY:V])
+        group_on_gpsimd(own_early[:, :, 2:4], own_high[:])
 
-        first = [[pair_tile("first%d%d" % (d, g), "first%d%d" % (d, g)) for g in range(2)] for d in range(NEIGHBOURS)]
-        for t in range(PACK):
-            fetch = fetch_on_vector if t < PACK - 1 else fetch_on_scalar
+        near = [keep.tile([P, PACK, V], BF16, name="near%d" % d, tag="near%d" % d) for d in range(NEIGHBOURS)]
+        for t in range(PACK - 1):
             for d in range(NEIGHBOURS):
-                fetch(first[d][t // 2][:, t % 2, :], t, pos_sb[d], 0, HALF)
+                fetch_on_vector(near[d][:, t, 0:HALF], t, pos_sb[d], 0, HALF)
+        for d, width in enumerate((HALF, V, V)):
+            fetch_on_scalar(near[d][:, PACK - 1, 0:width], PACK - 1, pos_sb[d], 0, width)
 
-        larger_first = keep.tile([P, 2, 2, HALF], BF16, name="larger_first", tag="own1")
+        larger_first = keep.tile([P, PACK, HALF], BF16, name="larger_first", tag="own_high")
         z_first = keep.tile([P, PACK, HALF], BF16, name="z_first", tag="z_first", align_bytes=64)
-        for g in range(2):
-            nc.vector.tensor_tensor(larger_first[:, g], first[0][g][:], first[1][g][:], MAX)
-        own_codes, own_plane = quantize("own", own_grouped[:, 0:EARLY, :], EARLY, "own_codes")
+        nc.vector.tensor_tensor(larger_first[:], near[0][:, :, 0:HALF], near[1][:, :, 0:HALF], MAX)
+        own_codes, own_plane = quantize("own", own_early[:], EARLY, "own_codes")
         for c in range(2):
             lo, hi = CHUNKS[c]
             second_product(c, W2, own_codes[:, lo:hi], own_plane[:, lo:hi])
-        for g in range(2):
-            nc.vector.tensor_tensor(z_first[:, 2 * g : 2 * g + 2, :], larger_first[:, g], first[2][g][:], MAX)
+        nc.vector.tensor_tensor(z_first[:], larger_first[:], near[2][:, :, 0:HALF], MAX)
         z_first_grouped = keep.tile([P, HALF, PACK], BF16, name="z_first_grouped", align_bytes=64)
         group_on_gpsimd(z_first_grouped[:], z_first[:])
 
-        low = [pair_tile("low0", "first21"), pair_tile("low1", "first20"), pair_tile("low2", "low2")]
-        high = [pair_tile("high%d" % d, "high%d" % d) for d in range(NEIGHBOURS)]
-        for d in range(2):
-            for t in range(2):
-                fetch_on_vector(low[d][:, t, :], t, pos_sb[d], HALF, V)
-        for d in range(NEIGHBOURS):
-            for t in range(2):
-                fetch_on_scalar(high[d][:, t, :], 2 + t, pos_sb[d], HALF, V)
-        for t in range(2):
-            fetch_on_scalar(low[2][:, t, :], t, pos_sb[2], HALF, V)
+        held = keep.tile([P, 3, HALF], BF16, name="held", tag="own_early", align_bytes=64)
+        for row, (t, d) in enumerate(((0, 0), (1, 0), (0, 2))):
+            fetch_on_vector(held[:, row, :], t, pos_sb[d], HALF, V)
+        for t, d in ((2, 0), (3, 0), (2, 1), (0, 1), (1, 1), (1, 2), (2, 2)):
+            fetch_on_scalar(near[d][:, t, HALF:V], t, pos_sb[d], HALF, V)
+
         own_last = keep.tile([P, 2, QUARTER], BF16, name="own_last")
         for t in range(2):
             fetch_on_scalar(own_last[:, t, :], 2 + t, cen_sb, EARLY, V)
-        group_with(nc.scalar.copy, own_grouped[:, EARLY:V, 2:4], own_last[:])
+        group_with(nc.scalar.copy, own_late[:, :, 2:4], own_last[:])
 
         codes, plane = quantize("z0", z_first_grouped[:], HALF, "z0_codes")
         second_product(0, W3, codes[:], plane[:])
-        larger_second = keep.tile([P, 2, 2, HALF], BF16, name="larger_second", tag="z_first", align_bytes=64)
+        larger_second = keep.tile([P, PACK, HALF], BF16, name="larger_second", tag="z_first", align_bytes=64)
         z_second = keep.tile([P, PACK, HALF], BF16, name="z_second", tag="z_second", align_bytes=64)
-        for g, rows in ((1, high), (0, low)):
-            nc.vector.tensor_tensor(larger_second[:, g], rows[0][:], rows[1][:], MAX)
-        nc.vector.tensor_tensor(z_second[:, 2:4, :], larger_second[:, 1], high[2][:], MAX)
+        nc.vector.tensor_tensor(larger_second[:, 2:4], near[0][:, 2:4, HALF:V], near[1][:, 2:4, HALF:V], MAX)
+        nc.vector.tensor_tensor(larger_second[:, 0:2], held[:, 0:2], near[1][:, 0:2, HALF:V], MAX)
+        nc.vector.tensor_tensor(z_second[:, 0], larger_second[:, 0], held[:, 2], MAX)
         quarters = [slice(u * QUARTER, (u + 1) * QUARTER) for u in range(2)]
+        third = near[2][:, :, HALF:V]
         for cols in quarters:
-            nc.vector.tensor_tensor(z_second[:, 0:2, cols], larger_second[:, 0, :, cols], low[2][:, :, cols], MAX)
-        store(0, nc.scalar.copy)
+            nc.vector.tensor_tensor(z_second[:, 1:4, cols], larger_second[:, 1:4, cols], third[:, 1:4, cols], MAX)
         z_second_grouped = []
         for u, cols in enumerate(quarters):
             grouped = keep.tile([P, QUARTER, PACK], BF16, name="z_second_grouped%d" % u, align_bytes=64)
             group_with(nc.vector.tensor_copy, grouped[:], z_second[:, :, cols])
             z_second_grouped.append(grouped)
+        store(0, nc.scalar.copy, "result0")
         codes, plane = quantize("z1", z_second_grouped[0][:], QUARTER, "z1_codes")
         second_product(1, W3, codes[:], plane[:])
-        store(1, nc.scalar.copy)
-        codes, plane = quantize("last", own_grouped[:, EARLY:V, :], QUARTER, "z_second")
+        store(1, nc.scalar.copy, "result1")
+        codes, plane = quantize("last", own_late[:], QUARTER, "z_second")
         second_product(2, W2, codes[:], plane[:])
         codes, plane = quantize("z2", z_second_grouped[1][:], QUARTER, "z2_codes")
         second_product(2, W3, codes[:], plane[:])
-        store(2, nc.vector.tensor_copy)
+        store(2, nc.vector.tensor_copy, "result2")

@@ -30,6 +30,7 @@ VECTOR_PIECES = (0, 1, 3)
 H_BANKS = 5
 HALF = V // 2
 QUARTER = V // 4
+SHARED = HALF + QUARTER
 EARLY = HALF + QUARTER
 CHUNKS = ((0, HALF), (HALF, EARLY), (EARLY, V))
 W2, W3 = 0, 1
@@ -172,10 +173,10 @@ def tile_picked_sagecat_max_p_kernel(
             for c, (lo, hi) in enumerate(CHUNKS)
         ]
 
-        def second_product(c, w, codes, plane):
+        def second_product(c, w, codes, plane, opens=W2):
             nc.tensor.matmul_mx(
                 out_acc[c][:], lhsT=tail_codes[:, w, :].bitcast(FP8X4), lhsT_scale=tail_planes[:, w, :],
-                rhs=codes.bitcast(FP8X4), rhs_scale=plane, start=w == W2, stop=w == W3,
+                rhs=codes.bitcast(FP8X4), rhs_scale=plane, start=w == opens, stop=w != opens,
             )
 
         def store(c, engine_copy, tag):
@@ -184,28 +185,29 @@ def tile_picked_sagecat_max_p_kernel(
             engine_copy(result[:], out_acc[c][:])
             nc.sync.dma_start(out[:, lo:hi], result[:])
 
-        own_early = keep.tile([P, EARLY, PACK], BF16, name="own_early", tag="own_early", align_bytes=64)
-        own_late = keep.tile([P, QUARTER, PACK], BF16, name="own_late", align_bytes=64)
+        own_grouped = keep.tile([P, V, PACK], BF16, name="own_grouped", align_bytes=64)
         own_low = keep.tile([P, 2, V], BF16, name="own_low")
         own_high = keep.tile([P, 2, EARLY], BF16, name="own_high", tag="own_high")
         for t in range(2):
             fetch_on_vector(own_low[:, t, :], t, cen_sb, 0, V)
             fetch_on_scalar(own_high[:, t, :], 2 + t, cen_sb, 0, EARLY)
-        group_on_gpsimd(own_early[:, :, 0:2], own_low[:, :, 0:EARLY])
-        group_on_gpsimd(own_late[:, :, 0:2], own_low[:, :, EARLY:V])
-        group_on_gpsimd(own_early[:, :, 2:4], own_high[:])
+        group_on_gpsimd(own_grouped[:, :, 0:2], own_low[:])
+        group_on_gpsimd(own_grouped[:, 0:EARLY, 2:4], own_high[:])
 
-        near = [keep.tile([P, PACK, V], BF16, name="near%d" % d, tag="near%d" % d) for d in range(NEIGHBOURS)]
+        near = [
+            keep.tile([P, PACK, width], BF16, name="near%d" % d, tag="near%d" % d) for d, width in enumerate((HALF, V, V))
+        ]
         for t in range(PACK - 1):
             for d in range(NEIGHBOURS):
-                fetch_on_vector(near[d][:, t, 0:HALF], t, pos_sb[d], 0, HALF)
+                end = SHARED if (t, d) == (2, 1) else HALF
+                fetch_on_vector(near[d][:, t, 0:end], t, pos_sb[d], 0, end)
         for d, width in enumerate((HALF, V, V)):
             fetch_on_scalar(near[d][:, PACK - 1, 0:width], PACK - 1, pos_sb[d], 0, width)
 
         larger_first = keep.tile([P, PACK, HALF], BF16, name="larger_first", tag="own_high")
         z_first = keep.tile([P, PACK, HALF], BF16, name="z_first", tag="z_first", align_bytes=64)
         nc.vector.tensor_tensor(larger_first[:], near[0][:, :, 0:HALF], near[1][:, :, 0:HALF], MAX)
-        own_codes, own_plane = quantize("own", own_early[:], EARLY, "own_codes")
+        own_codes, own_plane = quantize("own", own_grouped[:, 0:EARLY, :], EARLY, "own_codes")
         for c in range(2):
             lo, hi = CHUNKS[c]
             second_product(c, W2, own_codes[:, lo:hi], own_plane[:, lo:hi])
@@ -213,39 +215,49 @@ def tile_picked_sagecat_max_p_kernel(
         z_first_grouped = keep.tile([P, HALF, PACK], BF16, name="z_first_grouped", align_bytes=64)
         group_on_gpsimd(z_first_grouped[:], z_first[:])
 
-        held = keep.tile([P, 3, HALF], BF16, name="held", tag="own_early", align_bytes=64)
+        held = keep.tile([P, 3, HALF], BF16, name="held", tag="near0")
+        high_first = keep.tile([P, 2, HALF], BF16, name="high_first")
         for row, (t, d) in enumerate(((0, 0), (1, 0), (0, 2))):
             fetch_on_vector(held[:, row, :], t, pos_sb[d], HALF, V)
-        for t, d in ((2, 0), (3, 0), (2, 1), (0, 1), (1, 1), (1, 2), (2, 2)):
-            fetch_on_scalar(near[d][:, t, HALF:V], t, pos_sb[d], HALF, V)
-
+        for t in range(2):
+            fetch_on_scalar(near[1][:, t, HALF:V], t, pos_sb[1], HALF, V)
+        for t in range(2):
+            fetch_on_scalar(high_first[:, t, :], 2 + t, pos_sb[0], HALF, V)
+        for t, d, lo, hi in ((2, 1, SHARED, V), (1, 2, HALF, V), (2, 2, HALF, V)):
+            fetch_on_scalar(near[d][:, t, lo:hi], t, pos_sb[d], lo, hi)
         own_last = keep.tile([P, 2, QUARTER], BF16, name="own_last")
         for t in range(2):
             fetch_on_scalar(own_last[:, t, :], 2 + t, cen_sb, EARLY, V)
-        group_with(nc.scalar.copy, own_late[:, :, 2:4], own_last[:])
+        group_with(nc.scalar.copy, own_grouped[:, EARLY:V, 2:4], own_last[:])
 
-        codes, plane = quantize("z0", z_first_grouped[:], HALF, "z0_codes")
-        second_product(0, W3, codes[:], plane[:])
         larger_second = keep.tile([P, PACK, HALF], BF16, name="larger_second", tag="z_first", align_bytes=64)
         z_second = keep.tile([P, PACK, HALF], BF16, name="z_second", tag="z_second", align_bytes=64)
-        nc.vector.tensor_tensor(larger_second[:, 2:4], near[0][:, 2:4, HALF:V], near[1][:, 2:4, HALF:V], MAX)
         nc.vector.tensor_tensor(larger_second[:, 0:2], held[:, 0:2], near[1][:, 0:2, HALF:V], MAX)
+        nc.vector.tensor_tensor(larger_second[:, 2:4], high_first[:], near[1][:, 2:4, HALF:V], MAX)
         nc.vector.tensor_tensor(z_second[:, 0], larger_second[:, 0], held[:, 2], MAX)
-        quarters = [slice(u * QUARTER, (u + 1) * QUARTER) for u in range(2)]
         third = near[2][:, :, HALF:V]
-        for cols in quarters:
+
+        def largest(cols):
             nc.vector.tensor_tensor(z_second[:, 1:4, cols], larger_second[:, 1:4, cols], third[:, 1:4, cols], MAX)
-        z_second_grouped = []
-        for u, cols in enumerate(quarters):
-            grouped = keep.tile([P, QUARTER, PACK], BF16, name="z_second_grouped%d" % u, align_bytes=64)
+
+        def group_quarter(name, cols):
+            grouped = keep.tile([P, QUARTER, PACK], BF16, name=name, tag=name, align_bytes=64)
             group_with(nc.vector.tensor_copy, grouped[:], z_second[:, :, cols])
-            z_second_grouped.append(grouped)
-        store(0, nc.scalar.copy, "result0")
-        codes, plane = quantize("z1", z_second_grouped[0][:], QUARTER, "z1_codes")
+            return grouped
+
+        third_quarter, last_quarter = slice(0, QUARTER), slice(QUARTER, HALF)
+        codes, plane = quantize("z0", z_first_grouped[:], HALF, "z0_codes")
+        second_product(0, W3, codes[:], plane[:])
+        largest(third_quarter)
+        largest(last_quarter)
+        z_third_grouped = group_quarter("z_third_grouped", third_quarter)
+        z_last_grouped = group_quarter("z_last_grouped", last_quarter)
+        codes, plane = quantize("z1", z_third_grouped[:], QUARTER, "z1_codes")
         second_product(1, W3, codes[:], plane[:])
+        store(0, nc.scalar.copy, "result0")
         store(1, nc.scalar.copy, "result1")
-        codes, plane = quantize("last", own_late[:], QUARTER, "z_second")
-        second_product(2, W2, codes[:], plane[:])
-        codes, plane = quantize("z2", z_second_grouped[1][:], QUARTER, "z2_codes")
-        second_product(2, W3, codes[:], plane[:])
+        codes, plane = quantize("z2", z_last_grouped[:], QUARTER, "z2_codes")
+        second_product(2, W3, codes[:], plane[:], opens=W3)
+        codes, plane = quantize("last", own_grouped[:, EARLY:V, :], QUARTER, "z_second")
+        second_product(2, W2, codes[:], plane[:], opens=W3)
         store(2, nc.vector.tensor_copy, "result2")

from contextlib import ExitStack

import concourse.mybir as mybir

K, T, S, V, H, N = 512, 4096, 1024, 512, 512, 128
FLOPS = 2 * K * H * S + 2 * 2 * H * N * V

F32 = mybir.dt.float32
BF16 = mybir.dt.bfloat16
I32 = mybir.dt.int32
U32 = mybir.dt.uint32
U16 = mybir.dt.uint16
U8 = mybir.dt.uint8
FP8X4 = mybir.dt.float8_e4m3fn_x4
MAX = mybir.AluOpType.max
ADD = mybir.AluOpType.add
MULT = mybir.AluOpType.mult
COPY = mybir.ActivationFunctionType.Copy
RELU = mybir.ActivationFunctionType.Relu

P = 128
PACK = 4
QUADS = 4
LIST_ROWS = 16
NEIGHBOURS = 3
BANK = 512
X_HEAD = 1536
PIECES = ((256, 256, 256, 128, 128), (256, 256, 512), (512, 512), (512, 512))
VECTOR_PIECES = (0, 1, 3)
H_BANKS = 5
HALF = V // 2
QUARTER = V // 4
SHARED = HALF + QUARTER
EARLY = HALF + QUARTER
CHUNKS = ((0, HALF), (HALF, EARLY), (EARLY, V))
W2, W3 = 0, 1


def tile_picked_sagecat_max_p_kernel(
    tc, x_words, x_scales, w1, w2_words, w2_scales, w3_words, w3_scales, offs, cen, pos1, pos2, pos3, out
):
    nc = tc.nc
    with ExitStack() as ctx:
        keep = ctx.enter_context(tc.tile_pool(name="keep", bufs=1))
        psum_h = ctx.enter_context(tc.psum_pool(name="psum_h", bufs=H_BANKS))
        psum_out = ctx.enter_context(tc.psum_pool(name="psum_out", bufs=1))

        def load_list(name, source):
            tile = keep.tile(list(source.shape), U16, name=name)
            nc.sync.dma_start(tile[:], source)
            return tile

        def entries(tile, lo, hi):
            return tile[:, lo // LIST_ROWS : hi // LIST_ROWS]

        scale_table = keep.tile([P, T], U8, name="scale_table")
        nc.gpsimd.memset(scale_table[:, 0 : T // 2].bitcast(I32), 0)
        nc.vector.memset(scale_table[:, T // 2 : T].bitcast(I32), 0)
        idle = keep.tile([P, 16], F32, name="idle")
        nc.gpsimd.memset(idle[:, 0:8], 0.0)
        nc.scalar.activation(idle[:, 8:9], idle[:, 0:1], RELU)

        x_rows = x_words[0].rearrange("p n j -> p (n j)").bitcast(I32)
        x_table = keep.tile([P, T], U32, name="x_table")
        nc.sync.dma_start(x_table[:, 0:X_HEAD].bitcast(I32), x_rows[:, 0:X_HEAD])
        offs_sb = load_list("offs_sb", offs)
        nc.sync.dma_start(scale_table[32:96:4, :].bitcast(I32), x_scales[0].bitcast(I32))
        nc.sync.dma_start(x_table[:, X_HEAD:T].bitcast(I32), x_rows[:, X_HEAD:T])
        w1_rows = w1.rearrange("(p j) c -> p j c", j=PACK)
        w1_raw = keep.tile([P, PACK, H], F32, name="w1_raw", tag="w1_raw", align_bytes=64)
        for pair in range(2):
            nc.sync.dma_start(w1_raw[:, 2 * pair : 2 * pair + 2, :], w1_rows[:, 2 * pair : 2 * pair + 2, :])
        cen_sb = load_list("cen_sb", cen)
        pos_sb = [load_list("pos0_sb", pos1)]

        x_plane = keep.tile([P, S], U8, name="x_plane", align_bytes=64)
        nc.gpsimd.memset(x_plane[:].bitcast(I32), 0)

        picked_scales = keep.tile([P, S], U8, name="picked_scales", align_bytes=64)
        nc.vector.tensor_copy(picked_scales[:], scale_table[:].indirect(offs_sb[:]))
        for q in range(QUADS):
            nc.scalar.dma_start(
                x_plane[32 * q : 32 * q + 4, :].bitcast(I32),
                picked_scales[32 + 16 * q : 48 + 16 * q : 4, :].bitcast(I32),
            )

        pos_sb.extend([load_list("pos1_sb", pos2), load_list("pos2_sb", pos3)])
        x_codes = keep.tile([P, S], U32, name="x_codes", align_bytes=64)
        nc.vector.tensor_copy(x_codes[:], x_table[:].indirect(offs_sb[:]))

        w1_view = w1_raw[:].rearrange("p j (m t) -> p m t j", t=PACK)
        dealt = keep.tile([P, PACK, P, PACK], BF16, name="dealt", tag="dealt", align_bytes=64)
        dealt_view = dealt[:].rearrange("p t m j -> p m t j")
        w1_codes = keep.tile([P, PACK * P], U32, name="w1_codes", align_bytes=64)
        w1_plane = keep.tile([P, PACK * P], U8, name="w1_plane", align_bytes=64)

        def quantize_w1(first_tile, end_tile):
            cols = slice(first_tile * P, end_tile * P)
            source = dealt[:, first_tile:end_tile].rearrange("p t m j -> p (t m j)")
            nc.vector.quantize_mx(w1_codes[:, cols].bitcast(FP8X4), w1_plane[:, cols], source)

        def round_on_scalar(places, tiles, pair):
            nc.scalar.activation(dealt_view[:, places, tiles, pair], w1_view[:, places, tiles, pair], COPY)

        def round_on_gpsimd(places, tiles, pair):
            nc.gpsimd.tensor_scalar(
                dealt_view[:, places, tiles, pair], w1_view[:, places, tiles, pair], 1.0, 0.0, MULT, ADD
            )

        early, late = slice(0, 2), slice(2, 4)
        every, low, high = slice(0, P), slice(0, P // 2), slice(P // 2, P)
        round_on_scalar(every, slice(0, 2), early)
        round_on_gpsimd(every, slice(2, 4), early)
        round_on_scalar(low, 0, late)
        round_on_gpsimd(high, 0, late)
        round_on_scalar(every, 1, late)
        round_on_scalar(every, slice(2, 4), late)
        quantize_w1(0, 1)
        quantize_w1(1, 2)

        h = [keep.tile([P, S], F32, name="h%d" % t) for t in range(PACK)]
        for t in range(PACK):
            lo = 0
            for piece, width in enumerate(PIECES[t]):
                acc = psum_h.tile([P, width], F32, name="acc")
                nc.tensor.matmul_mx(
                    acc[:],
                    lhsT=w1_codes[:, t * P : (t + 1) * P].bitcast(FP8X4),
                    lhsT_scale=w1_plane[:, t * P : (t + 1) * P],
                    rhs=x_codes[:, lo : lo + width].bitcast(FP8X4),
                    rhs_scale=x_plane[:, lo : lo + width],
                    start=True,
                    stop=True,
                )
                if t == 0 and piece in VECTOR_PIECES:
                    nc.vector.tensor_scalar_max(h[t][:, lo : lo + width], acc[:], 0.0)
                else:
                    nc.scalar.activation(h[t][:, lo : lo + width], acc[:], RELU)
                lo = lo + width
                if t == 0 and piece == 3:
                    quantize_w1(2, 4)

        tail_codes = keep.tile([P, 2, N], U32, name="tail_codes", tag="w1_raw", align_bytes=64)
        tail_planes = keep.tile([P, 2, N], U8, name="tail_planes", tag="dealt", align_bytes=64)
        nc.gpsimd.memset(tail_planes[:].rearrange("p w n -> p (w n)").bitcast(I32), 0)
        for w, words, scales in ((W2, w2_words, w2_scales), (W3, w3_words, w3_scales)):
            nc.sync.dma_start(tail_codes[:, w, :].bitcast(I32), words[0].rearrange("p n j -> p (n j)").bitcast(I32))
            for q in range(QUADS):
                nc.sync.dma_start(
                    tail_planes[32 * q : 32 * q + 4, w, :].bitcast(I32), scales[0, 4 * q : 4 * q + 4, :].bitcast(I32)
                )

        def fetch_on_vector(dst, t, lst, lo, hi):
            nc.vector.tensor_copy(dst, h[t][:].indirect(entries(lst, lo, hi)))

        def fetch_on_scalar(dst, t, lst, lo, hi):
            nc.scalar.activation(dst, h[t][:].indirect(entries(lst, lo, hi)), COPY)

        def group_on_gpsimd(grouped, rows):
            nc.gpsimd.tensor_scalar(grouped, rows.rearrange("p t v -> p v t"), 1.0, 0.0, MULT, ADD)

        def group_with(engine_copy, grouped, rows):
            engine_copy(grouped.rearrange("p (c i) t -> p c t i", i=4), rows.rearrange("p t (c i) -> p c t i", i=4))

        def quantize(name, grouped, width, tag):
            codes = keep.tile([P, width], U32, name=name + "_codes", tag=tag, align_bytes=64)
            plane = keep.tile([P, width], U8, name=name + "_plane", align_bytes=64)
            nc.vector.quantize_mx(codes[:].bitcast(FP8X4), plane[:], grouped.rearrange("p v t -> p (v t)"))
            return codes, plane

        out_acc = [
            psum_out.tile([P, hi - lo], F32, name="out_acc%d" % c, tag="out_acc%d" % c)
            for c, (lo, hi) in enumerate(CHUNKS)
        ]

        def second_product(c, w, codes, plane, opens=W2):
            nc.tensor.matmul_mx(
                out_acc[c][:], lhsT=tail_codes[:, w, :].bitcast(FP8X4), lhsT_scale=tail_planes[:, w, :],
                rhs=codes.bitcast(FP8X4), rhs_scale=plane, start=w == opens, stop=w != opens,
            )

        def store(c, engine_copy, tag):
            lo, hi = CHUNKS[c]
            result = keep.tile([P, hi - lo], F32, name="result%d" % c, tag=tag)
            engine_copy(result[:], out_acc[c][:])
            nc.sync.dma_start(out[:, lo:hi], result[:])

        own_grouped = keep.tile([P, V, PACK], BF16, name="own_grouped", align_bytes=64)
        own_low = keep.tile([P, 2, V], BF16, name="own_low")
        own_high = keep.tile([P, 2, EARLY], BF16, name="own_high", tag="own_high")
        for t in range(2):
            fetch_on_vector(own_low[:, t, :], t, cen_sb, 0, V)
            fetch_on_scalar(own_high[:, t, :], 2 + t, cen_sb, 0, EARLY)
        group_on_gpsimd(own_grouped[:, :, 0:2], own_low[:])
        group_on_gpsimd(own_grouped[:, 0:EARLY, 2:4], own_high[:])

        near = [
            keep.tile([P, PACK, width], BF16, name="near%d" % d, tag="near%d" % d) for d, width in enumerate((HALF, V, V))
        ]
        for t in range(PACK - 1):
            for d in range(NEIGHBOURS):
                end = SHARED if (t, d) == (2, 1) else HALF
                fetch_on_vector(near[d][:, t, 0:end], t, pos_sb[d], 0, end)
        for d, width in enumerate((HALF, V, V)):
            fetch_on_scalar(near[d][:, PACK - 1, 0:width], PACK - 1, pos_sb[d], 0, width)

        larger_first = keep.tile([P, PACK, HALF], BF16, name="larger_first", tag="own_high")
        z_first = keep.tile([P, PACK, HALF], BF16, name="z_first", tag="z_first", align_bytes=64)
        nc.vector.tensor_tensor(larger_first[:], near[0][:, :, 0:HALF], near[1][:, :, 0:HALF], MAX)
        own_codes, own_plane = quantize("own", own_grouped[:, 0:EARLY, :], EARLY, "own_codes")
        for c in range(2):
            lo, hi = CHUNKS[c]
            second_product(c, W2, own_codes[:, lo:hi], own_plane[:, lo:hi])
        nc.vector.tensor_tensor(z_first[:], larger_first[:], near[2][:, :, 0:HALF], MAX)
        z_first_grouped = keep.tile([P, HALF, PACK], BF16, name="z_first_grouped", align_bytes=64)
        group_on_gpsimd(z_first_grouped[:], z_first[:])

        held = keep.tile([P, 3, HALF], BF16, name="held", tag="near0")
        high_first = keep.tile([P, 2, HALF], BF16, name="high_first")
        for row, (t, d) in enumerate(((0, 0), (1, 0), (0, 2))):
            fetch_on_vector(held[:, row, :], t, pos_sb[d], HALF, V)
        for t in range(2):
            fetch_on_scalar(near[1][:, t, HALF:V], t, pos_sb[1], HALF, V)
        for t in range(2):
            fetch_on_scalar(high_first[:, t, :], 2 + t, pos_sb[0], HALF, V)
        for t, d, lo, hi in ((2, 1, SHARED, V), (1, 2, HALF, V), (2, 2, HALF, V)):
            fetch_on_scalar(near[d][:, t, lo:hi], t, pos_sb[d], lo, hi)
        own_last = keep.tile([P, 2, QUARTER], BF16, name="own_last")
        for t in range(2):
            fetch_on_scalar(own_last[:, t, :], 2 + t, cen_sb, EARLY, V)
        group_with(nc.scalar.copy, own_grouped[:, EARLY:V, 2:4], own_last[:])

        larger_second = keep.tile([P, PACK, HALF], BF16, name="larger_second", tag="z_first", align_bytes=64)
        z_second = keep.tile([P, PACK, HALF], BF16, name="z_second", tag="z_second", align_bytes=64)
        nc.vector.tensor_tensor(larger_second[:, 0:2], held[:, 0:2], near[1][:, 0:2, HALF:V], MAX)
        nc.vector.tensor_tensor(larger_second[:, 2:4], high_first[:], near[1][:, 2:4, HALF:V], MAX)
        nc.vector.tensor_tensor(z_second[:, 0], larger_second[:, 0], held[:, 2], MAX)
        third = near[2][:, :, HALF:V]

        def largest(cols):
            nc.vector.tensor_tensor(z_second[:, 1:4, cols], larger_second[:, 1:4, cols], third[:, 1:4, cols], MAX)

        def group_quarter(name, cols):
            grouped = keep.tile([P, QUARTER, PACK], BF16, name=name, tag=name, align_bytes=64)
            group_with(nc.vector.tensor_copy, grouped[:], z_second[:, :, cols])
            return grouped

        third_quarter, last_quarter = slice(0, QUARTER), slice(QUARTER, HALF)
        codes, plane = quantize("z0", z_first_grouped[:], HALF, "z0_codes")
        second_product(0, W3, codes[:], plane[:])
        largest(third_quarter)
        largest(last_quarter)
        z_third_grouped = group_quarter("z_third_grouped", third_quarter)
        z_last_grouped = group_quarter("z_last_grouped", last_quarter)
        codes, plane = quantize("z1", z_third_grouped[:], QUARTER, "z1_codes")
        second_product(1, W3, codes[:], plane[:])
        store(0, nc.scalar.copy, "result0")
        store(1, nc.scalar.copy, "result1")
        codes, plane = quantize("z2", z_last_grouped[:], QUARTER, "z2_codes")
        second_product(2, W3, codes[:], plane[:], opens=W3)
        codes, plane = quantize("last", own_grouped[:, EARLY:V, :], QUARTER, "z_second")
        second_product(2, W2, codes[:], plane[:], opens=W3)
        store(2, nc.vector.tensor_copy, "result2")
